import numpy as np, ml_dtypes
CORES = [24,48,72,152,176,200]
N = 6
BF = ml_dtypes.bfloat16
W, H, LG = 4096, 2048, 12
B, I, RO, A, C, DS = 16, 192, 6, 1, 5, (3,)
def pick(p, x):
    return np.take_along_axis(p, x, 3)
def swap(p, s, t):
    p = np.array(p); a = np.array(p[..., t:B * I:B])
    m = np.array(np.broadcast_to(B * np.arange(I) + (s[:, :, :1] & (B - 1)), a.shape))
    b = np.take_along_axis(p, m, 3); np.put_along_axis(p, m, a, 3); p[..., t:B * I:B] = b
    return p
def shuffled(rng):
    return rng.permuted(np.tile(np.arange(W), (N, 8, 16, 1)), axis=3)
def lanes(rng):
    return rng.integers(0, W, (N, 8, 16, I))
def join(p, s, t):
    return {"pm": (p[..., :H] + W * p[..., H:]).reshape(N, 128, H).astype(np.int32), "sa": s.reshape(N, 128, I).astype(np.int32), "ta": t.reshape(N, 128, I).astype(np.int32)}
def halves(pm):
    w = np.asarray(pm).astype(np.int64); return np.concatenate([w & (W - 1), w >> LG], axis=-1)
def setup_inputs(rng):
    return join(shuffled(rng), lanes(rng), lanes(rng))
def setup_inputs_spread(rng):
    size = np.exp2(rng.integers(0, 14, (N, 8, 16, 1)))
    p = np.argsort(np.arange(W) + size * rng.random((N, 8, 16, W)), axis=3)
    s, t = [(np.exp2(LG * rng.random((N, 8, 1, I))) * rng.random((N, 8, 16, I))).astype(np.int64) for _ in range(2)]
    return join(p, s, t)
def setup_inputs_ends(rng):
    ty = (np.arange(8)[:, None] + 1 + ((np.arange(16) + 1) % 16) // 4) % 2
    p = np.zeros((N, 8, 16, W), np.int64); end, low, n = B * (I - 1), 2 * B, len(DS)
    for v in (0, 1):
        big, small = (end, low) if v == 0 else (low, end)
        at = {big: W - 1, small: 0, end - H: W - 2 if v == 0 else 1}
        x = [W - 2 - j for j in range(n + 2)]; y = [0] + [j + 2 for j in range(n + 1)]
        at.update(zip(x, x[1:] + [big - 1])); at.update(zip(y, y[1:] + [small - 1]))
        a = np.array([c for c in at]); b = np.array([at[c] for c in at])
        ra = np.setdiff1d(np.arange(W), a); rb = np.setdiff1d(np.arange(W), b); q = np.zeros((N * int(np.count_nonzero(ty == v)), W), np.int64)
        q[:, a] = b; q[:, ra] = rng.permuted(np.tile(rb, (len(q), 1)), axis=1)
        p[:, ty == v] = q.reshape(N, -1, W)
    s = (W - 1) * rng.integers(0, 2, (N, 8, 16, I)); t = (W - 1) * rng.integers(0, 2, (N, 8, 16, I)); top = (W - 1) * (ty == 0)
    s[..., I - 1] = top; t[..., I - 1] = top; s[..., 2] = W - 1 - top; t[..., 2] = W - 1 - top
    return join(p, s, t)
def setup_inputs_corners(rng):
    p = shuffled(rng); x = np.arange(W)
    for r in range(N):
        kind = rng.permutation(8)
        for g in range(8):
            c = kind[g]
            if c == 5: p[r, g] = rng.permuted(x.reshape(W // B, B), axis=1).reshape(W)
            elif c == 6: p[r, g] = np.array(p[r, g, 0])
            elif c < 5: p[r, g] = (x, W - 1 - x, (x + 1) & (W - 1), (x - 1) & (W - 1), x ^ 1)[c]
    u = p[..., 0:B * I:B]; z = rng.integers(0, 4, (N, 8, 16, I))
    aim = np.where(z == 0, 0, np.where(z == 1, W - 1, np.where(z == 2, B * np.arange(I), lanes(rng))))
    mode = ((np.arange(N)[:, None] + np.arange(8)) % 4)[:, :, None]
    dig = np.where(mode == 0, 0, np.where(mode == 1, B - 1, np.where(mode == 2, 1, rng.integers(0, B, (N, 8, I)))))
    back = np.argsort(p[:, :, 0], axis=2)
    aim[:, :, 0] = np.take_along_axis(back, B * rng.integers(0, W // B, (N, 8, I)) + dig, 2)
    return join(p, (aim - u) & (W - 1), rng.choice(np.array([0, 1, W - 2, W - 1]), (N, 8, 16, I)))
def setup_inputs_crowd(rng):
    p = shuffled(rng); place = rng.integers(0, W, (N, 8, 16, 1)); aim = np.array(np.broadcast_to(place, (N, 8, 16, I)))
    i = int(rng.integers(0, I)); aim[:, 1::4, :, i] = (aim[:, 1::4, :, i] + 1) & (W - 1)
    aim[:, 2::4] = (W - 1) * rng.integers(0, 2, (N, 2, 16, I)); aim[:, 3::4] = place[:, 3::4, :1]
    t = np.array(np.broadcast_to(rng.integers(0, W, (N, 8, 1, 1)), (N, 8, 16, I)))
    return join(p, (aim - p[..., 0:B * I:B]) & (W - 1), t)
def setup_inputs_calm(rng):
    p = shuffled(rng); s = lanes(rng); n = W // B
    a = B * rng.permuted(np.tile(np.arange(n), (N, 8, B, 1)), axis=3) + rng.permuted(np.tile(np.arange(B), (N, 8, 1)), axis=2)[..., None]
    p[:, :, 0] = a.swapaxes(2, 3).reshape(N, 8, W)
    lone = np.arange(I) == rng.integers(0, I, (N, 8, 1))
    s[:, :, 0] = B * (s[:, :, 0] // B) + rng.integers(0, B, (N, 8, 1))
    s[:, 1::2, 0] ^= lone[:, 1::2].astype(np.int64)
    q, w, hist, back = p, s, [], []
    for t in range(RO):
        if t: w = np.roll(w, (A, C), axis=(0, 1))
        h = np.roll(q, (-A * t, -C * t), axis=(0, 1)); x = np.zeros_like(h)
        np.put_along_axis(x, h, np.broadcast_to(np.arange(W), h.shape), 3); hist.append(h); back.append(x)
        if t < RO - 1: w = pick(q, (w + q[..., t:B * I:B]) & (W - 1)); q = swap(q, w, t)
    g = np.arange(8)[:, None, None]; r = np.arange(N)[:, None, None, None]; j = (g >> 1) + 4 * r
    full = (g & 1) == 1; top = (W - 1) * (j & 1); few = (g + r) & 3
    when = np.array(np.broadcast_to(np.where(full, 1 + (j >> 1) % (RO - 1), 1 + np.arange(I) % (RO - 1)), (N, 8, 16, I)))
    want = np.where(rng.random((N, 8, 16, I)) < 0.5, few, W - 1 - (few & 1))
    for t in range(1, RO):
        e = hist[t][..., t:B * I:B]
        for v in (0, W - 1):
            m = (e == v) & ~full; when = np.where(m, t - 1, when); want = np.where(m, v, want)
    when = np.where(full & ((r & 1) == 1) & lone[:, :, None, :], RO, when)
    b = lanes(rng)
    for t in range(RO - 1, -1, -1):
        y = (pick(back[t], np.array(np.broadcast_to(top, (N, 8, 16, 1)))) - 1) & (W - 1)
        for d in DS[::-1]:
            y = pick(np.roll(back[t], -d, axis=0), y)
        y = pick(back[t], y)
        b = np.where(when == t, np.where(full, y, want), b)
        b = (pick(back[t], b) - hist[t][..., t:B * I:B]) & (W - 1)
    b[:, :, 0] = s[:, :, 0]
    w, zs = b, []
    for t in range(RO):
        w = pick(hist[t], (w + hist[t][..., t:B * I:B]) & (W - 1)); v = pick(hist[t], w)
        for d in DS:
            v = pick(np.roll(hist[t], -d, axis=0), v)
        zs.append(pick(hist[t], (v + 1) & (W - 1)))
    c = lanes(rng)
    for t in range(RO - 1, -1, -1):
        u = pick(back[t], c) - zs[t]; c = lanes(rng)
        for k in range(15, 0, -1):
            c[:, :, k] = (u[:, :, k] - c[:, :, (k + 1) & 15]) & (W - 1)
        c = np.where(full & (when == t), top, c)
    return join(p, b, np.where(full, c, rng.integers(0, 4, (N, 8, 16, I))))
def check_inputs(d):
    bad = []
    for k, lo, hi in (("pm", 1, W * W - 2), ("sa", 0, W - 1), ("ta", 0, W - 1)):
        if np.min(d[k]) < lo or np.max(d[k]) > hi: bad.append("range of " + k)
    if np.any(np.sort(halves(d["pm"]), axis=-1) != np.arange(W)): bad.append("permutations in pm")
    return bad
def reference(pm, sa, ta):
    P = halves(pm).reshape(N, 8, 16, W); S = sa.astype(np.int64).reshape(N, 8, 16, I); T = ta.astype(np.int64).reshape(N, 8, 16, I)
    for t in range(RO):
        if t:
            S = np.roll(S, (A, C), axis=(0, 1)); T = np.roll(T, (A, C), axis=(0, 1))
        S = pick(P, (S + P[..., t:B * I:B]) & (W - 1))
        z = pick(P, S)
        for a in DS:
            z = pick(np.roll(P, -a, axis=0), z)
        z = pick(P, (z + 1) & (W - 1))
        T = pick(P, (T + np.roll(T, -1, axis=2) + z) & (W - 1))
        if t < RO - 1: P = swap(P, S, t)
    return {"ys": S.reshape(N, 128, I).astype(np.float32), "yt": T.reshape(N, 128, I).astype(np.float32)}

@@ -1,0 +1,634 @@
+import numpy as np
+from concourse.mybir import AluOpType as AL, ActivationFunctionType as AF
+
+W, H, B, NI, RO, GS, DQ = 4096, 2048, 16, 192, 6, 5, 3
+MID = 2048.0
+CFG = dict(NB=3, CH=[0, 96, 192], PIECE=48, ZS=True, SS=True, TS=True, NG=8, LD=[0, 512, 1024, 1536, 2048], AH=[0, 1, 2], look=0.15, seed=0, jit=0.0,
+           cg=1.56, cs=3.8, hop=3.2, rel=6.0, pe=0.42, pool="",
+           CV=2, PC=512, VQ="P", MS=1, MT=1, CHX={}, MAXP=96,
+           DC=0, wake=0.1, iss=0.3, CUT={}, PRI=None, ON=None, TQ="P", sb=30.0, slope=0.0, BIAS=[0.0] * 30)
+C3 = [0, 64, 128, 192]
+CFG.update(NB=4, LD=[0, 256, 768, 1408, 2048], AH=[], look=0.06, cg=1.6, cs=4.5, hop=3.5, rel=6.3, wake=0.18,
+           iss=0.7, pool="w", PC=384, slope=11.02,
+           CHX={1: C3, 2: C3, 3: C3, 43: C3, 52: C3, 53: C3, 54: C3, 55: C3, 45: C3, 44: C3},
+           CUT={96: [(54, "A"), (42, "V")], 64: [(34, "A"), (30, "V")], 128: [(70, "A"), (58, "V")]},
+           BIAS=[-3.1, -26.6, -50.0, -64.0, 1.6, 22.7, 18.6, -5.9, 1.2, -7.2, -0.2, -6.2, 33.8, -37.8, 2.9, -29.4, -36.5,
+                 -7.4, 0.5, 27.5, 0.2, -14.6, -2.3, -17.3, -16.9, -1.2, -60.1, -26.3, 36.3, -13.6])
+
+SCRATCH = {
+    "one": ("sbuf", [128, 128], "bfloat16"), "kt": ("sbuf", [128, NI], "bfloat16"), "ks": ("sbuf", [128, NI], "bfloat16"),
+    "pmb": ("sbuf", [128, H], "int32"), "sab": ("sbuf", [128, NI], "int32"), "tab": ("sbuf", [128, NI], "int32"),
+    "dm": ("sbuf", [128, 16 + 2048], "bfloat16"), "eye2": ("sbuf", [128, 256], "bfloat16"),
+    "rot2": ("sbuf", [128, 256], "bfloat16"), "eye32": ("sbuf", [128, 128], "float32"),
+    "b0": ("sbuf", [128, 12], "int32"), "b1": ("sbuf", [128, 12], "int32"), "base": ("sbuf", [128, 12], "int32"),
+    "a32": ("sbuf", [128, RO * NI], "float32"), "b32": ("sbuf", [128, RO * NI], "int32"),
+    "m1": ("sbuf", [128, RO * NI], "int32"), "m5": ("sbuf", [128, RO * NI], "int32"),
+    "dt": ("sbuf", [128, RO * 16], "int32"), "dl": ("sbuf", [128, RO * 16], "uint16"),
+    "oys": ("sbuf", [128, NI], "float32"), "oyt": ("sbuf", [128, NI], "float32"),
+}
+for _n in ("off1", "off2", "off5", "zout", "zin", "zret", "zback"):
+    SCRATCH[_n] = ("sbuf", [128, RO * NI], "uint16")
+for _n in ("so", "si", "to", "ti"):
+    SCRATCH[_n] = ("sbuf", [128, RO * NI], "float16")
+for _i in range(CFG["NB"]):
+    SCRATCH["tb%d" % _i] = ("sbuf", [128, W + 8], "int32")
+for _i in range(CFG["NG"]):
+    SCRATCH["gb%d" % _i] = ("sbuf", [128, B * NI], "float16")
+for _i in range(8):
+    SCRATCH["ps%d" % _i] = ("psum", [128, 512], "float32")
+
+
+def nominal(c):
+    return dict(f=1.25, cg=c["cg"], cs=c["cs"], pe=c["pe"], fix=0.05, wake=c["wake"], iss=c["iss"], hop=c["hop"], rel=c["rel"],
+                first=2.0, dma0=2.0, bw=300.0)
+
+
+def cost(o, q, m):
+    k, n = o["k"], o["n"]
+    cy = 0.00083 * m["f"]
+    if k == "gather":
+        d = (0.05 if q == "V" else 0.065) + n * m["cg"] * cy
+    elif k == "scatter":
+        d = 0.05 + n * m["cs"] * cy
+    elif k == "ew":
+        d = (0.17 + 2 * n * cy) if q == "P" else m["fix"] + max(64, n) * cy
+    elif k == "mm":
+        d = n * m["pe"] * 0.001 * m["f"]
+    elif k == "send":
+        hold = m["iss"] + m["first"] * o.get("first", 0)
+        return hold, hold + m[o["via"]] + m["first"] * o.get("first2", 0)
+    elif k == "dma":
+        return (n / m["bw"] * 0.001 if o.get("own") else 0.1), m["dma0"] + n / m["bw"] * 0.001
+    return d, d + m["wake"]
+
+
+def build(c):
+    ops = []
+    CH = list(zip(c["CH"][:-1], c["CH"][1:]))
+    NB = c["NB"]
+
+    def op(name, q, k, n, deps, **kw):
+        o = dict(name=name, q=q, k=k, n=n, deps=[d for d in deps if d is not None], pre=[], i=len(ops))
+        o.update(kw)
+        ops.append(o)
+        return o
+
+    def ew(name, q, n, deps, **kw):
+        return op(name, q, "ew", n, deps, **kw)
+
+    FL = "AV"
+    z1 = ew("zero_dm", "V", 1032, [], do=("zero_dm",))
+    z2 = ew("zero_eye", "V", 128, [], do=("zero_eye",))
+    dm = ew("dm", "P", 2048, [z1], do=("dm",))
+    io0 = ew("io0", "P", 12, [], do=("io0",))
+    io1 = ew("io1", "P", 12, [], do=("io1",))
+    ba = ew("ba", "V", 12, [io0], do=("ba",))
+    base = ew("base", "V", 24, [ba, io1], do=("base",))
+    eye = ew("eye", "P", 256, [z2], do=("eye",))
+    eye32 = ew("eye32", "P", 128, [eye], do=("eye32",))
+    rot0 = ew("rot0", "P", 256, [eye], do=("rot0",))
+    rot = ew("rot", "P", 16, [rot0], do=("rot",))
+    LD = list(zip(c["LD"][:-1], c["LD"][1:]))
+    lds, un = [], []
+    for j, (x, y) in enumerate(LD):
+        lds.append(op("ld%d" % j, "S", "dma", 512 * y, [], do=("ld", x, y), sem="ld%d" % j))
+    lsa = op("ldsa", "S", "dma", 512 * H + 98304, [], do=("ldsa",), sem="ldsa")
+    lta = op("ldta", "S", "dma", 512 * H + 196608, [], do=("ldta",), sem="ldta")
+    for x, y in zip(lds + [lsa], lds[1:] + [lsa, lta]):
+        y["pre"].append(x)
+    for j, (x, y) in enumerate(LD):
+        un.append((x, y, ew("lo%d" % j, "V", y - x, [lds[j]], do=("lo", x, y))))
+        if j in c["AH"]:
+            h = ew("hj%d" % j, "A", y - x, [lds[j]], do=("hj", x, y))
+            un.append((H + x, H + y, ew("hk%d" % j, FL, y - x, [h], do=("hk", x, y))))
+        else:
+            un.append((H + x, H + y, ew("hi%d" % j, "V", y - x, [lds[j]], do=("hi", x, y))))
+    made = {0: [o for _, _, o in un]}
+    start = {0: made[0]}
+    copied = lambda v: v >= c["CV"]
+    for b in range(1, NB):
+        start[b] = [ew("cp%d_%d" % (b, x), c["TQ"] if copied(b) else FL, 512, [o for u, v, o in un if u < x + 512 and x < v],
+                       do=("cp", b, 0, x, x + 512)) for x in range(B * NI if copied(b) else 0, W, 512)]
+    one = ew("one", "V", 64, [], do=("one",))
+    k0 = ew("k0", "V", 64, [], do=("k0",))
+    k1 = ew("k1", "V", 64, [k0], do=("k1",))
+    k2 = ew("k2", "V", 64, [], do=("k2",))
+
+    def chunks(t, st):
+        x = c["CHX"].get(10 * t + st, c["CH"])
+        return list(zip(x[:-1], x[1:]))
+
+    def over(parts, a, b):
+        return [o for x, y, o in parts if x < b and a < y]
+    t16 = ew("t16", FL, NI, [lta], do=("t16",))
+    readers = {v: [] for v in range(RO)}
+    for b in range(1, NB):
+        readers[0] += start[b]
+    wrap, a32, bg, dl = {}, {}, {}, {}
+    sarr, tarr = {}, {}
+    first = [True]
+
+    def pieces(name, t, st, a, b, deps, win):
+        out = []
+        x = a
+        cut = c["CUT"].get(b - a) or [(c["PIECE"], FL)] * NI
+        while x < b:
+            y = min(b, x + cut[len(out)][0])
+            o = op("%s_%d" % (name, x), cut[len(out)][1], "gather", B * (y - x), deps + made[t], stage=(t, st), cols=(x, y), win=win)
+            readers[t].append(o)
+            out.append(o)
+            x = y
+        return out
+
+    def ext(name, t, st, a, b, gs, last=True):
+        return op(name, "E", "mm", B * max(64, b - a), gs + [dm], stage=(t, st), cols=(a, b), bank=name, do=("ext", last))
+
+    def sends(kind, t, split, srcs, via):
+        res = []
+        for a, b in ([(x, y) for x, y, _ in srcs] if split else [(0, NI)]):
+            o = op("send_%s%d_%d" % (kind, t, a), "P", "send", 0, over(srcs, a, b), via=via,
+                   do=("send", kind, t, a, b), sem="%s%d_%d" % (kind, t, a))
+            res.append((a, b, o))
+        return res
+
+    def remainder(nm, t, a, b, src, bank, buf, off, add, short):
+        if short:
+            i1 = ew(nm + "a", "V", b - a, [src], rb=bank, do=("quot", buf, t, a, b))
+            return ew(nm + "b", "V", b - a, [i1], rb=bank, do=("rem", buf, off, t, a, b))
+        i1 = ew(nm + "a", FL, b - a, [src], rb=bank, do=("conv", buf, t, a, b, add))
+        i2 = ew(nm + "b", "V", b - a, [i1], do=("and", buf, t, a, b))
+        return ew(nm + "c", "P" if "u" in c["pool"] else FL, b - a, [i2], do=("tou", buf, off, t, a, b))
+
+    def bring(v):
+        b = v % NB
+        lo = max(0, v - NB)
+        prev = list(start[b]) if v < NB else readers[v - NB]
+        if copied(v):
+            lo = v - 1
+            pc = c["PC"]
+            cps = []
+            for x in range(0, B * NI, pc):
+                kw = dict(do=("cp", b, (v - 1) % NB, x, x + pc), late=prev)
+                if x < c["DC"]:
+                    cps.append(op("vc%d_%d" % (v, x), "S", "dma", 512 * pc, made[v - 1], sem="vc%d_%d" % (v, x), own=1, **kw))
+                else:
+                    cps.append(ew("vc%d_%d" % (v, x), c["VQ"], pc, made[v - 1], **kw))
+            readers[v - 1] += cps
+            prev = cps
+        if lo == v - 1 and NB > 1:
+            x = lo
+            cc = op("bcol%d" % x, FL, "gather", NI, [dl[x]] + made[x], do=("bcol", x, b), late=prev)
+            readers[x].append(cc)
+            made[v] = [op("scat%d_%d" % (x, v), "V", "scatter", NI, [dl[x], a32[x], cc], do=("scat", x, b))]
+            return
+        for x in range(lo, v):
+            if x not in bg:
+                bg[x] = op("bg%d" % x, FL, "gather", NI, [dl[x]] + made[x], do=("bg", x))
+                readers[x].append(bg[x])
+            sc = op("scat%d_%d" % (x, v), "V", "scatter", NI, [dl[x], a32[x]], do=("scat", x, b), late=prev)
+            cc = ew("col%d_%d" % (x, v), "P" if "c" in c["pool"] else FL, NI, [sc, bg[x]], do=("col", x, b))
+            prev = []
+            sc["deps"] += [] if x == lo else [last]
+            last = cc
+        made[v] = [last]
+
+    for t in range(RO):
+        if t:
+            bring(t)
+        wrap[t] = ew("wrap%d" % t, "P" if "w" in c["pool"] and t else FL, 1, made[t], do=("wrap", t % NB))
+        readers[t].append(wrap[t])
+        if t or RO > 1:
+            a32[t] = ew("a32_%d" % t, "P" if "a" in c["pool"] and t else FL, NI, made[t], do=("a32", t))
+            readers[t].append(a32[t])
+        g1, c1u, c1h, c2, c3, c4, c5 = [], [], [], [], [], [], []
+        for a, b in chunks(t, 1):
+            nm = "%d_%d" % (t, a)
+            if t == 0:
+                need = over(un, B * a, B * b)
+                i1 = ew("i1a" + nm, "V", 2 * (b - a), [lsa] + need, do=("sum0", a, b))
+                readers[0].append(i1)
+                i2 = ew("i1b" + nm, "V", b - a, [i1], do=("and", "m1", t, a, b))
+                i3 = ew("i1c" + nm, FL, b - a, [i2], do=("tou", "m1", "off1", t, a, b))
+            else:
+                ms = op("mms" + nm, "E", "mm", (5 + c["MS"]) * max(64, b - a), over(sarr[t], a, b) + [a32[t], eye, eye32, one, k2],
+                        bank="mms" + nm, do=("mms", t, a, b))
+                i3 = remainder("i1" + nm, t, a, b, ms, ms["bank"], "m1", "off1", MID, c["MS"])
+            gs = pieces("g1_%d" % t, t, 1, a, b, [i3], ("off1", W))
+            g1 += gs
+            e = ext("e1" + nm, t, 1, a, b, gs)
+            if t < RO - 1:
+                h = ew("c1h" + nm, FL, b - a, [e], rb=e["bank"], do=("conv", "so", t, a, b, 0.0))
+            else:
+                h = ew("c1h" + nm, FL, b - a, [e], rb=e["bank"], do=("conv", "oys", 0, a, b, MID))
+            u = ew("c1u" + nm, FL, b - a, [e], rb=e["bank"], do=("conv", "off2", t, a, b, MID))
+            c1u.append((a, b, u)); c1h.append((a, b, h))
+        if t < RO - 1:
+            sarr[t + 1] = sends("s", t + 1, c["SS"], c1h, "rel")
+            dmm = op("dmm%d" % t, "E", "mm", B * 64, g1 + [dm], stage=(t, 1), bank="dmm%d" % t, do=("dmm",))
+            d1 = ew("d1_%d" % t, FL, 12, [dmm], rb=dmm["bank"], do=("d1", t))
+            d2 = ew("d2_%d" % t, "V", 12, [d1], do=("d2", t))
+            dl[t] = ew("d3_%d" % t, "V", 24, [d2, base], do=("d3", t))
+        else:
+            op("stys", "S", "dma", 98304, over(c1h, 0, NI), do=("st", "ys", 0, NI), sem="stys")
+        for a, b in chunks(t, 2):
+            nm = "%d_%d" % (t, a)
+            e = ext("e2" + nm, t, 2, a, b, pieces("g2_%d" % t, t, 2, a, b, over(c1u, a, b), ("off2", W)))
+            c2.append((a, b, ew("c2" + nm, FL, b - a, [e], rb=e["bank"], do=("conv", "zout", t, a, b, MID))))
+        za = sends("z", t, c["ZS"], c2, "hop")
+        for a, b in chunks(t, 3):
+            nm = "%d_%d" % (t, a)
+            e = ext("e3" + nm, t, 3, a, b, pieces("g3_%d" % t, t, 3, a, b, over(za, a, b), ("zin", W)))
+            c3.append((a, b, ew("c3" + nm, FL, b - a, [e], rb=e["bank"], do=("conv", "zret", t, a, b, MID + 1))))
+        zb = sends("y", t, c["ZS"], c3, "hop")
+        for a, b in chunks(t, 4):
+            nm = "%d_%d" % (t, a)
+            src = over(tarr[t], a, b) if t else [t16]
+            e = ext("e4" + nm, t, 4, a, b, pieces("g4_%d" % t, t, 4, a, b, over(zb, a, b) + [wrap[t]], ("zback", W + 1)), last=False)
+            e["pre"] += src
+            mt = op("mmt" + nm, "E", "mm", (1 + c["MT"]) * max(64, b - a), src + [rot, one, k1, e], same=e, rb=e["bank"], do=("mmt", t, a, b))
+            c4.append((a, b, remainder("i5" + nm, t, a, b, mt, e["bank"], "m5", "off5", 3 * MID, c["MT"])))
+        for a, b in chunks(t, 5):
+            nm = "%d_%d" % (t, a)
+            e = ext("e5" + nm, t, 5, a, b, pieces("g5_%d" % t, t, 5, a, b, over(c4, a, b), ("off5", W)))
+            if t < RO - 1:
+                c5.append((a, b, ew("c5" + nm, FL, b - a, [e], rb=e["bank"], do=("conv", "to", t, a, b, 0.0))))
+            else:
+                x = ew("c5" + nm, FL, b - a, [e], rb=e["bank"], do=("conv", "oyt", 0, a, b, MID))
+                op("styt%d" % a, "S", "dma", 512 * (b - a), [x], do=("st", "yt", a, b), sem="styt%d" % a)
+        if t < RO - 1:
+            tarr[t + 1] = sends("t", t + 1, c["TS"], c5, "rel")
+    for o in ops:
+        o["deps"] = o["deps"] + list(o.get("late", []))
+    return ops
+
+
+def schedule(c):
+    ops = build(c)
+    m = nominal(c)
+    rs = np.random.RandomState(c["seed"])
+    users = [[] for _ in ops]
+    for o in ops:
+        for d in o["deps"]:
+            users[d["i"]].append(o)
+    order, left = [], [len(o["deps"]) for o in ops]
+    todo = [o for o in ops if not o["deps"]]
+    while todo:
+        o = todo.pop()
+        order.append(o)
+        for u in users[o["i"]]:
+            left[u["i"]] -= 1
+            if not left[u["i"]]:
+                todo.append(u)
+    for o in reversed(order):
+        o["pr"] = cost(o, o["q"][0], m)[1] + max([u["pr"] for u in users[o["i"]]] + [0.0])
+    for o in ops:
+        o["pr"] += c["jit"] * float(rs.rand())
+        if o["k"] == "gather" and "stage" in o:
+            o["pr"] += c["BIAS"][5 * o["stage"][0] + o["stage"][1] - 1] - c["slope"] * o["cols"][0] / NI
+        elif o.get("do", ("",))[0] != "cp":
+            o["pr"] += c["sb"]
+    if c["PRI"]:
+        for o in ops:
+            o["pr"] = -c["PRI"][o["i"]]
+            o["q"] = c["ON"][o["i"]] if c["ON"] else o["q"]
+    guse, buse = {}, {}
+    for o in ops:
+        if "stage" in o:
+            guse.setdefault(o["stage"], []).append(o)
+        for key in ("bank", "rb"):
+            if key in o:
+                buse.setdefault(o[key], []).append(o)
+    gslot, bslot = {}, {}
+    gown, bown = [None] * c["NG"], [None] * 8
+    free = {q: 0.0 for q in "AVPES"}
+    left = [len(o["deps"]) for o in ops]
+    ready = [o for o in ops if not o["deps"]]
+    done = []
+
+    def pick(own, use):
+        best = None
+        for s, w in enumerate(own):
+            us = [] if w is None else use[w]
+            if all("t1" in u for u in us):
+                tt = max([u["t1"] for u in us] + [0.0])
+                if best is None or tt < best[0]:
+                    best = (tt, s, us)
+        return best
+
+    def earliest(o):
+        if any("t1" not in p for p in o["pre"]):
+            return None
+        r = max([(d["te"] if d is o.get("same") else d["t1"]) for d in o["deps"]] + [0.0])
+        extra, take = [], None
+        if o["k"] == "gather" and "stage" in o:
+            if o["stage"] not in gslot:
+                p = pick(gown, guse)
+                if p is None:
+                    return None
+                take = ("g", p[1]); extra = [u for u in p[2] if u["k"] == "mm"]
+            else:
+                extra = gslot[o["stage"]][1]
+        if "bank" in o:
+            p = pick(bown, buse)
+            if p is None:
+                return None
+            take = ("b", p[1]); extra = p[2]
+        if "rb" in o and "same" not in o:
+            extra = [u for u in buse[o["rb"]] if "t1" in u]
+        r = max([r] + [u["t1"] for u in extra])
+        return r, extra, take
+
+    while ready:
+        cand = []
+        for o in ready:
+            e = earliest(o)
+            if e is not None:
+                for q in o["q"]:
+                    cand.append((max(e[0], free[q]), q, o, e))
+        t0, q0 = min((x[0], x[1]) for x in cand)
+        _, q, o, e = max((x for x in cand if x[1] == q0 and x[0] <= t0 + c["look"]), key=lambda x: (x[2]["pr"], -x[2]["i"]))
+        o["on"] = q
+        if o["k"] == "send":
+            o["first"] = int(not any(x["k"] == "send" for x in done))
+            o["first2"] = int(o["via"] == "rel" and not any(x.get("via") == "rel" for x in done))
+        o["t0"] = max(e[0], free[q])
+        hold, fin = cost(o, q, m)
+        o["te"], o["t1"] = o["t0"] + hold, o["t0"] + fin
+        free[q] = o["te"]
+        o["deps"] = o["deps"] + [u for u in e[1] if all(u is not d for d in o["deps"])]
+        if e[2] is not None:
+            if e[2][0] == "g":
+                gown[e[2][1]] = o["stage"]; gslot[o["stage"]] = (e[2][1], e[1])
+            else:
+                bown[e[2][1]] = o["bank"]; bslot[o["bank"]] = e[2][1]
+        ready = [x for x in ready if x is not o]
+        done.append(o)
+        for u in users[o["i"]]:
+            left[u["i"]] -= 1
+            if not left[u["i"]]:
+                ready.append(u)
+    for o in done:
+        if "stage" in o:
+            o["g"] = gslot[o["stage"]][0]
+        for key in ("bank", "rb"):
+            if key in o:
+                o["ps"] = bslot[o[key]]
+    last, into, out = {}, {}, []
+    done.sort(key=lambda x: x["t0"])
+    for o in done:
+        p = last.get(o["on"])
+        if (p is not None and o["k"] == "gather" and p["k"] == "gather" and "stage" in o and o.get("stage") == p.get("stage")
+                and p["cols"][1] == o["cols"][0] and all(d["t1"] <= p["t0"] + 1e-9 for d in o["deps"])
+                and p["n"] + o["n"] <= B * c.get("MAXP", 96)):
+            p["cols"] = (p["cols"][0], o["cols"][1]); p["n"] += o["n"]
+            p["deps"] = p["deps"] + [d for d in o["deps"] if all(d is not x for x in p["deps"])]
+            into[o["i"]] = p
+            continue
+        last[o["on"]] = o
+        out.append(o)
+    for o in out:
+        ds = []
+        for d in o["deps"]:
+            d = into.get(d["i"], d)
+            if all(d is not x for x in ds):
+                ds.append(d)
+        o["deps"] = ds
+    return out
+
+
+def timing(plan, m):
+    free = {q: 0.0 for q in "AVPES"}
+    te, t1, busy = {}, {}, []
+    for o in plan:
+        s = max([free[o["on"]]] + [(te if d is o.get("same") else t1)[d["i"]] for d in o["deps"]])
+        hold, fin = cost(o, o["on"], m)
+        if o.get("own"):
+            busy.append((s, s + hold))
+        if o["k"] == "send":
+            fin += max([y - s - hold for x, y in busy if x < s + hold < y] + [0.0])
+        te[o["i"]], t1[o["i"]] = s + hold, s + fin
+        free[o["on"]] = s + hold
+    return max(t1.values())
+
+
+PLAN = schedule(CFG)
+SEMAPHORES = ["qA", "qV", "qP", "qE", "left"] + [o["sem"] for o in PLAN if "sem" in o]
+LAND = {"z": ("zout", "zin"), "y": ("zret", "zback"), "s": ("so", "si"), "t": ("to", "ti")}
+
+
+def low_engines(topo, src, dst):
+    m = topo.mask(src, dst)
+    return m, len(topo.engines(src, dst))
+
+
+def relay_of(topo, T, src, dst):
+    if topo.may_write(src, dst):
+        return None
+    return [x for x in topo.cores_of(src) if T.rank_of(x) is None and topo.die(x) == topo.die(src) and topo.may_write(x, dst)][0]
+
+
+def rank_program(g, core, T, topo):
+    N = len(T.cores)
+    S = T.sem
+    rank = T.rank_of(core)
+    if rank is None:
+        for r in range(N):
+            src, dst = T.cores[r], T.cores[(r + 1) % N]
+            if relay_of(topo, T, src, dst) == core:
+                mask, ne = low_engines(topo, core, dst)
+                nin = low_engines(topo, src, T.cores[(r + DQ) % N])[1]
+                rid, pid = topo.addr(dst, core)
+                tot = 0
+                for o in PLAN:
+                    if o["k"] == "send" and o["via"] == "rel":
+                        _, kind, t, a, b = o["do"]
+                        ap = T[LAND[kind][1]][:, t * NI + a:t * NI + b]
+                        g.wait_ge(S[o["sem"]], nin)
+                        g.remote_dma(ap, ap, S[o["sem"]], S.left, pid, rid, mask)
+                        tot += ne
+                g.wait_ge(S.left, tot)
+        return
+    nxt, prv, par = T.cores[(rank + 1) % N], T.cores[(rank - 1) % N], T.cores[(rank + DQ) % N]
+    mask, ne = low_engines(topo, core, par)
+    rel = relay_of(topo, T, core, nxt)
+    rin = relay_of(topo, T, prv, core)
+    to = {"hop": par, "rel": nxt if rel is None else rel}
+    gain = {"hop": low_engines(topo, par, core)[1], "rel": low_engines(topo, prv if rin is None else rin, core)[1]}
+    Q = {"A": g.scalar, "V": g.vector, "P": g, "E": g.tensor, "S": g.sync}
+    V, PE = g.vector, g.tensor
+    NB = CFG["NB"]
+
+    def sl(name, t, a, b):
+        return T[name][:, t * NI + a:t * NI + b]
+
+    def affine(q, out, in_, add):
+        if q == "A":
+            return g.scalar.activation(out, in_, AF.Identity, bias=float(add)) if add else g.scalar.activation(out, in_, AF.Copy)
+        if q == "P":
+            return g.affine_select(out, in_, [[0, int(out.shape[1])]], AL.is_ge, 0.0, 0, 0)
+        return V.tensor_scalar(out, in_, float(add), None, AL.add) if add else V.tensor_copy(out, in_)
+
+    def emit(o):
+        q = o["on"]
+        if o["k"] == "gather" and "stage" in o:
+            t, (a, b), (off, w) = o["stage"][0], o["cols"], o["win"]
+            return affine(q, T["gb%d" % o["g"]][:, B * a:B * b], T["tb%d" % (t % NB)][:, 0:w].indirect(sl(off, t, a, b)), -MID)
+        d = o["do"]
+        k = d[0]
+        ps = T["ps%d" % o["ps"]] if "ps" in o else None
+        if k == "zero_dm":
+            return V.memset(T.dm[:], 0.0)
+        if k == "zero_eye":
+            return V.memset(T.eye2[:], 0.0)
+        if k == "dm":
+            return g.affine_select(T.dm[:, 16:], T.dm[:, 16:], [[-1024, 16], [-16, 8], [1023, 16]], AL.not_equal, 1.0, 0, 1)
+        if k == "io0":
+            return g.iota(T.b0[:], [[0, 12]], 0, B)
+        if k == "io1":
+            return g.iota(T.b1[:], [[B * B, 12]], 0, 0)
+        if k == "ba":
+            return V.tensor_scalar(T.b0[:], T.b0[:], B * B - 1, None, AL.bitwise_and)
+        if k == "base":
+            return V.tensor_tensor(T.base[:], T.b0[:], T.b1[:], AL.add)
+        if k == "eye":
+            return g.affine_select(T.eye2[:], T.eye2[:], [[0, 2], [-1, 128]], AL.not_equal, 1.0, 0, 1)
+        if k == "eye32":
+            return affine("P", T.eye32[:], T.eye2[:, 0:128], 0)
+        if k == "rot0":
+            return g.affine_select(T.rot2[:], T.eye2[:], [[0, 2], [-1, 128]], AL.not_equal, 1.0, -1, 1)
+        if k == "rot":
+            return g.affine_select(T.rot2[:, 15:256:16], T.eye2[:, 15:256:16], [[0, 2], [-16, 8]], AL.not_equal, 1.0, 0, 1)
+        if k == "ld":
+            return g.sync.dma_start(T.pmb[:, d[1]:d[2]], T.pm[:, d[1]:d[2]])
+        if k == "ldsa":
+            return g.sync.dma_start(T.sab[:], T.sa[:])
+        if k == "ldta":
+            return g.sync.dma_start(T.tab[:], T.ta[:])
+        if k == "st":
+            return g.sync.dma_start(T[d[1]][:, d[2]:d[3]], T["o" + d[1]][:, d[2]:d[3]])
+        if k == "lo":
+            return V.tensor_scalar(T.tb0[:, d[1]:d[2]], T.pmb[:, d[1]:d[2]], W - 1, None, AL.bitwise_and)
+        if k == "hi":
+            return V.tensor_scalar(T.tb0[:, H + d[1]:H + d[2]], T.pmb[:, d[1]:d[2]], 12, None, AL.logical_shift_right)
+        if k == "hj":
+            return g.scalar.activation(T.tb0[:, H + d[1]:H + d[2]], T.pmb[:, d[1]:d[2]], AF.Identity,
+                                       bias=2.0 ** -13 + 0.5 - MID, scale=1.0 / W)
+        if k == "hk":
+            return affine(q, T.tb0[:, H + d[1]:H + d[2]], T.tb0[:, H + d[1]:H + d[2]], MID - 1)
+        if k == "cp" and q == "S":
+            return g.sync.dma_start(T["tb%d" % d[1]][:, d[3]:d[4]], T["tb%d" % d[2]][:, d[3]:d[4]])
+        if k == "cp":
+            return affine(q, T["tb%d" % d[1]][:, d[3]:d[4]], T["tb%d" % d[2]][:, d[3]:d[4]], 0)
+        if k == "one":
+            return V.memset(T.one[0:2, :], 1.0)
+        if k == "k0":
+            return V.memset(T.kt[0:2, :], 0.25)
+        if k == "k1":
+            return V.memset(T.kt[0:1, :], 3 * MID + W)
+        if k == "k2":
+            return V.memset(T.ks[0:1, :], MID)
+        if k == "quot":
+            _, name, t, a, b = d
+            if name == "m1":
+                return V.tensor_scalar(sl(name, t, a, b), ps[:, 0:b - a], float(W), float(W), AL.is_ge, AL.mult)
+            return V.tensor_scalar(sl(name, t, a, b), ps[:, 0:b - a], 2.0 ** 35 - MID, 2.0 ** 35, AL.add, AL.subtract)
+        if k == "rem":
+            _, name, off, t, a, b = d
+            return V.tensor_tensor(sl(off, t, a, b), ps[:, 0:b - a], sl(name, t, a, b), AL.subtract)
+        if k == "t16":
+            return affine(q, sl("ti", 0, 0, NI), T.tab[:], -MID)
+        if k == "wrap":
+            tb = T["tb%d" % d[1]]
+            return affine(q, tb[:, W:W + 1], tb[:, 0:1], 0)
+        if k == "a32":
+            return affine(q, sl("a32", d[1], 0, NI), T["tb%d" % (d[1] % NB)][:, d[1]:B * NI:B], 0)
+        if k == "sum0":
+            return V.tensor_tensor(sl("m1", 0, d[1], d[2]), T.sab[:, d[1]:d[2]], T.tb0[:, B * d[1]:B * d[2]:B], AL.add)
+        if k == "mms":
+            _, t, a, b = d
+            PE.matmul(ps[:, 0:b - a], T.eye2[:, 128 - B * GS:256 - B * GS], sl("si", t, a, b), True, False)
+            if CFG["MS"]:
+                PE.matmul(ps[:, 0:b - a], T.one[0:1, :], T.ks[0:1, 0:b - a], False, False)
+            return PE.matmul(ps[:, 0:b - a], T.eye32[:], sl("a32", t, a, b), False, True)
+        if k == "mmt":
+            _, t, a, b = d
+            x = 128 - B * GS if t else 0
+            if CFG["MT"]:
+                PE.matmul(ps[:, 0:b - a], T.one[0:2, :], T.kt[0:2, 0:b - a], False, False)
+            return PE.matmul(ps[:, 0:b - a], T.rot2[:, x:x + 128], sl("ti", t, a, b), False, True)
+        if k == "ext":
+            a, b = o["cols"]
+            for j in range(B):
+                r = PE.matmul(ps[:, 0:b - a], T.dm[:, 16 + 128 * j:144 + 128 * j], T["gb%d" % o["g"]][:, B * a + j:B * b:B],
+                              j == 0, d[1] and j == B - 1)
+            return r
+        if k == "dmm":
+            for j in range(B):
+                r = PE.matmul(ps[:, 0:12], T.dm[:, 16 - j:144 - j], T["gb%d" % o["g"]][:, B * j:B * NI:B * B], j == 0, j == B - 1)
+            return r
+        if k == "toint" or k == "conv":
+            _, name, t, a, b, add = d
+            return affine(q, sl(name, t, a, b), ps[:, 0:b - a], add)
+        if k == "and":
+            ap = sl(d[1], d[2], d[3], d[4])
+            return V.tensor_scalar(ap, ap, W - 1, None, AL.bitwise_and)
+        if k == "tou":
+            return affine(q, sl(d[2], d[3], d[4], d[5]), sl(d[1], d[3], d[4], d[5]), 0)
+        t = d[1]
+        if k == "d1":
+            return affine(q, T.dt[:, 16 * t:16 * t + 12], ps[:, 0:12], MID)
+        if k == "d2":
+            ap = T.dt[:, 16 * t:16 * t + 12]
+            return V.tensor_scalar(ap, ap, B - 1, None, AL.bitwise_and)
+        if k == "d3":
+            return V.tensor_tensor(T.dl[:, 16 * t:16 * t + 12], T.dt[:, 16 * t:16 * t + 12], T.base[:], AL.add)
+        if k == "bg":
+            return affine(q, sl("b32", t, 0, NI), T["tb%d" % (t % NB)][:, 0:W].indirect(T.dl[:, 16 * t:16 * t + 12]), 0)
+        if k == "bcol":
+            return affine(q, T["tb%d" % d[2]][:, t:B * NI:B], T["tb%d" % (t % NB)][:, 0:W].indirect(T.dl[:, 16 * t:16 * t + 12]), 0)
+        if k == "scat":
+            return V.tensor_copy(T["tb%d" % d[2]][:, 0:W].indirect(T.dl[:, 16 * t:16 * t + 12]), sl("a32", t, 0, NI))
+        if k == "col":
+            return affine(q, T["tb%d" % d[2]][:, t:B * NI:B], sl("b32", t, 0, NI), 0)
+        raise ValueError(k)
+
+    count = {q: 0 for q in "AVPE"}
+    mark, clock = {}, {}
+    known = {q: {} for q in Q}
+    waited = set()
+    sent = 0
+
+    def wait(q, name, val, ck):
+        if known[q].get(name, 0) < val:
+            Q[q].wait_ge(S[name], val)
+            waited.add((name, val))
+            known[q][name] = val
+            for n2, v2 in ck.items():
+                if known[q].get(n2, 0) < v2:
+                    known[q][n2] = v2
+
+    for o in PLAN:
+        q = o["on"]
+        for d in sorted(o["deps"], key=lambda x: -x["t1"]):
+            if d is not o.get("same"):
+                wait(q, mark[d["i"]][0], mark[d["i"]][1], clock[d["i"]])
+        if o["k"] == "send":
+            _, kind, t, a, b = o["do"]
+            ts = t - 1 if o["via"] == "rel" else t
+            rid, pid = topo.addr(to[o["via"]], core)
+            g.remote_dma(sl(LAND[kind][1], t, a, b), sl(LAND[kind][0], ts, a, b), S[o["sem"]], S.left, pid, rid, mask)
+            sent += ne
+            mark[o["i"]], clock[o["i"]] = (o["sem"], gain[o["via"]]), {}
+        elif o["k"] == "dma":
+            emit(o).then_inc(S[o["sem"]], 16)
+            mark[o["i"]], clock[o["i"]] = (o["sem"], 16), dict(known[q])
+        else:
+            emit(o).then_inc(S["q" + q], 1)
+            count[q] += 1
+            mark[o["i"]], clock[o["i"]] = ("q" + q, count[q]), dict(known[q])
+    g.wait_ge(S.left, sent)
+    for q in "AVPE":
+        g.wait_ge(S["q" + q], count[q])
+    for o in PLAN:
+        if "sem" in o and mark[o["i"]] not in waited:
+            g.sync.wait_ge(S[o["sem"]], mark[o["i"]][1])

@@ -1,28 +1,32 @@
-import numpy as np
 from concourse.mybir import AluOpType as AL, ActivationFunctionType as AF
 
 W, H, B, NI, RO, GS, DQ = 4096, 2048, 16, 192, 6, 5, 3
 MID = 2048.0
-CFG = dict(NB=3, CH=[0, 96, 192], PIECE=48, ZS=True, SS=True, TS=True, NG=8, LD=[0, 512, 1024, 1536, 2048], AH=[0, 1, 2], look=0.15, seed=0, jit=0.0,
-           cg=1.56, cs=3.8, hop=3.2, rel=6.0, pe=0.42, pool="",
-           CV=2, PC=512, VQ="P", MS=1, MT=1, CHX={}, MAXP=96,
-           DC=0, wake=0.1, iss=0.3, CUT={}, PRI=None, ON=None, TQ="P", sb=30.0, slope=0.0, BIAS=[0.0] * 30)
-C3 = [0, 64, 128, 192]
-CFG.update(NB=4, LD=[0, 256, 768, 1408, 2048], AH=[], look=0.06, cg=1.6, cs=4.5, hop=3.5, rel=6.3, wake=0.18,
-           iss=0.7, pool="w", PC=384, slope=11.02,
-           CHX={1: C3, 2: C3, 3: C3, 43: C3, 52: C3, 53: C3, 54: C3, 55: C3, 45: C3, 44: C3},
-           CUT={96: [(54, "A"), (42, "V")], 64: [(34, "A"), (30, "V")], 128: [(70, "A"), (58, "V")]},
-           BIAS=[-3.1, -26.6, -50.0, -64.0, 1.6, 22.7, 18.6, -5.9, 1.2, -7.2, -0.2, -6.2, 33.8, -37.8, 2.9, -29.4, -36.5,
-                 -7.4, 0.5, 27.5, 0.2, -14.6, -2.3, -17.3, -16.9, -1.2, -60.1, -26.3, 36.3, -13.6])
+BIG = 1.5 * 2.0 ** 19
+NB, NG, PIECE = 4, 8, 512
+FORM = {"2": [(0, 96), (96, 192)], "3": [(0, 64), (64, 128), (128, 192)], "m": [(64, 128), (0, 64), (128, 192)]}
+CFG = dict(
+    LD=[0, 256, 512, 1024, 1408, 1792, 2048], SA=2, AH=[0, 2],
+    ST={1: ("2", 0, 1), 2: ("2", 2, 2), 3: ("2", 7, 2), 4: ("2", 13, 2), 5: ("2", 16, 2)},
+    SH={1: 0.52, 2: 0.54, 3: 0.52, 4: 0.5, 5: 0.54},
+    AT={1: ("m", -17.0, 0.25), 2: ("2", -9.5, 1.5), 3: ("2", 6.5, 1.5), 51: ("2", 49.5, 0.25), 52: ("2", 52.0, 3.0),
+        44: ("2", 55.0, 0.25), 53: ("3", 55.5, 2.0), 45: ("3", 57.0, 2.0), 54: ("3", 63.0, 1.5), 55: ("3", 70.0, 1.5)},
+    PAT=dict(q1a=("A", -2.45), r1a=("V", -1.4), c1ua=("V", 1.6), d1=("A", 2.65), c1ub=("A", 2.8), c1ha=("V", 3.5),
+             d2=("V", 3.51), d3=("V", 4.65), bcol=("A", 4.65), c2a=("V", 4.75), c2b=("A", 5.5), scat=("V", 5.55),
+             c3a=("V", 9.55), c3b=("V", 11.8), q5a=("A", 14.75), r5a=("V", 15.5), q5b=("V", 16.55), r5b=("V", 16.8),
+             c5a=("V", 18.55), c5b=("A", 21.7)),
+    ON=dict(c1h="V", c1u="V", c2="V", c3="V", c5="AV", q1="A", q5="V", d1="V", bcol="A"),
+    wait=dict(cp=0.06, d1=0.8, send=0.8, bcol=0.2, conv=0.06, d2=0.2, half=0.5), lookp=0.05,
+    f=1.15, cg=1.5, cs=3.8, pe=0.45, wake=0.12, iss=0.3, hop=1.5, rel=3.0, first=0.8, dma0=1.6, bw=250.0)
 
 SCRATCH = {
-    "one": ("sbuf", [128, 128], "bfloat16"), "kt": ("sbuf", [128, NI], "bfloat16"), "ks": ("sbuf", [128, NI], "bfloat16"),
+    "one": ("sbuf", [128, 128], "bfloat16"), "kc": ("sbuf", [128, NI], "bfloat16"), "m0": ("sbuf", [128, NI], "int32"),
     "pmb": ("sbuf", [128, H], "int32"), "sab": ("sbuf", [128, NI], "int32"), "tab": ("sbuf", [128, NI], "int32"),
     "dm": ("sbuf", [128, 16 + 2048], "bfloat16"), "eye2": ("sbuf", [128, 256], "bfloat16"),
-    "rot2": ("sbuf", [128, 256], "bfloat16"), "eye32": ("sbuf", [128, 128], "float32"),
+    "rot2": ("sbuf", [128, 256], "bfloat16"), "eye32": ("sbuf", [128, 256], "float32"),
+    "mi": ("sbuf", [128, B], "int32"), "mk": ("sbuf", [128, B], "float32"),
     "b0": ("sbuf", [128, 12], "int32"), "b1": ("sbuf", [128, 12], "int32"), "base": ("sbuf", [128, 12], "int32"),
-    "a32": ("sbuf", [128, RO * NI], "float32"), "b32": ("sbuf", [128, RO * NI], "int32"),
-    "m1": ("sbuf", [128, RO * NI], "int32"), "m5": ("sbuf", [128, RO * NI], "int32"),
+    "m1": ("sbuf", [128, RO * NI], "bfloat16"), "m5": ("sbuf", [128, RO * NI], "bfloat16"),
     "dt": ("sbuf", [128, RO * 16], "int32"), "dl": ("sbuf", [128, RO * 16], "uint16"),
     "oys": ("sbuf", [128, NI], "float32"), "oyt": ("sbuf", [128, NI], "float32"),
 }
@@ -30,45 +34,39 @@ for _n in ("off1", "off2", "off5", "zout", "zin", "zret", "zback"):
     SCRATCH[_n] = ("sbuf", [128, RO * NI], "uint16")
 for _n in ("so", "si", "to", "ti"):
     SCRATCH[_n] = ("sbuf", [128, RO * NI], "float16")
-for _i in range(CFG["NB"]):
-    SCRATCH["tb%d" % _i] = ("sbuf", [128, W + 8], "int32")
-for _i in range(CFG["NG"]):
+for _i in range(NB + 1):
+    SCRATCH["tb%d" % _i] = ("sbuf", [128, W + 8], "float32" if _i else "int32")
+for _i in range(NG):
     SCRATCH["gb%d" % _i] = ("sbuf", [128, B * NI], "float16")
 for _i in range(8):
     SCRATCH["ps%d" % _i] = ("psum", [128, 512], "float32")
 
 
-def nominal(c):
-    return dict(f=1.25, cg=c["cg"], cs=c["cs"], pe=c["pe"], fix=0.05, wake=c["wake"], iss=c["iss"], hop=c["hop"], rel=c["rel"],
-                first=2.0, dma0=2.0, bw=300.0)
-
-
-def cost(o, q, m):
-    k, n = o["k"], o["n"]
+def cost(o, m):
+    k, n, q = o["k"], o["n"], o["q"]
     cy = 0.00083 * m["f"]
     if k == "gather":
         d = (0.05 if q == "V" else 0.065) + n * m["cg"] * cy
     elif k == "scatter":
         d = 0.05 + n * m["cs"] * cy
     elif k == "ew":
-        d = (0.17 + 2 * n * cy) if q == "P" else m["fix"] + max(64, n) * cy
+        d = (0.17 + 2 * n * cy) if q == "P" else 0.04 + max(64, n) * cy
     elif k == "mm":
         d = n * m["pe"] * 0.001 * m["f"]
     elif k == "send":
-        hold = m["iss"] + m["first"] * o.get("first", 0)
-        return hold, hold + m[o["via"]] + m["first"] * o.get("first2", 0)
+        hold = m["iss"] + m["first"] * o["first"]
+        return hold, hold + m[o["via"]] + m["first"] * o["first2"]
     elif k == "dma":
-        return (n / m["bw"] * 0.001 if o.get("own") else 0.1), m["dma0"] + n / m["bw"] * 0.001
+        return 0.1, m["dma0"] + n / m["bw"] * 0.001
     return d, d + m["wake"]
 
 
 def build(c):
     ops = []
-    CH = list(zip(c["CH"][:-1], c["CH"][1:]))
-    NB = c["NB"]
+    ON = c["ON"]
 
     def op(name, q, k, n, deps, **kw):
-        o = dict(name=name, q=q, k=k, n=n, deps=[d for d in deps if d is not None], pre=[], i=len(ops))
+        o = dict(name=name, q=q, k=k, n=n, deps=list(deps), pre=None, i=len(ops), pos=-1.0)
         o.update(kw)
         ops.append(o)
         return o
@@ -76,339 +74,255 @@ def build(c):
     def ew(name, q, n, deps, **kw):
         return op(name, q, "ew", n, deps, **kw)
 
-    FL = "AV"
-    z1 = ew("zero_dm", "V", 1032, [], do=("zero_dm",))
-    z2 = ew("zero_eye", "V", 128, [], do=("zero_eye",))
-    dm = ew("dm", "P", 2048, [z1], do=("dm",))
-    io0 = ew("io0", "P", 12, [], do=("io0",))
-    io1 = ew("io1", "P", 12, [], do=("io1",))
-    ba = ew("ba", "V", 12, [io0], do=("ba",))
-    base = ew("base", "V", 24, [ba, io1], do=("base",))
-    eye = ew("eye", "P", 256, [z2], do=("eye",))
-    eye32 = ew("eye32", "P", 128, [eye], do=("eye32",))
-    rot0 = ew("rot0", "P", 256, [eye], do=("rot0",))
-    rot = ew("rot", "P", 16, [rot0], do=("rot",))
-    LD = list(zip(c["LD"][:-1], c["LD"][1:]))
-    lds, un = [], []
-    for j, (x, y) in enumerate(LD):
-        lds.append(op("ld%d" % j, "S", "dma", 512 * y, [], do=("ld", x, y), sem="ld%d" % j))
-    lsa = op("ldsa", "S", "dma", 512 * H + 98304, [], do=("ldsa",), sem="ldsa")
-    lta = op("ldta", "S", "dma", 512 * H + 196608, [], do=("ldta",), sem="ldta")
-    for x, y in zip(lds + [lsa], lds[1:] + [lsa, lta]):
-        y["pre"].append(x)
-    for j, (x, y) in enumerate(LD):
-        un.append((x, y, ew("lo%d" % j, "V", y - x, [lds[j]], do=("lo", x, y))))
-        if j in c["AH"]:
-            h = ew("hj%d" % j, "A", y - x, [lds[j]], do=("hj", x, y))
-            un.append((H + x, H + y, ew("hk%d" % j, FL, y - x, [h], do=("hk", x, y))))
-        else:
-            un.append((H + x, H + y, ew("hi%d" % j, "V", y - x, [lds[j]], do=("hi", x, y))))
-    made = {0: [o for _, _, o in un]}
-    start = {0: made[0]}
-    copied = lambda v: v >= c["CV"]
-    for b in range(1, NB):
-        start[b] = [ew("cp%d_%d" % (b, x), c["TQ"] if copied(b) else FL, 512, [o for u, v, o in un if u < x + 512 and x < v],
-                       do=("cp", b, 0, x, x + 512)) for x in range(B * NI if copied(b) else 0, W, 512)]
-    one = ew("one", "V", 64, [], do=("one",))
-    k0 = ew("k0", "V", 64, [], do=("k0",))
-    k1 = ew("k1", "V", 64, [k0], do=("k1",))
-    k2 = ew("k2", "V", 64, [], do=("k2",))
-
-    def chunks(t, st):
-        x = c["CHX"].get(10 * t + st, c["CH"])
-        return list(zip(x[:-1], x[1:]))
-
     def over(parts, a, b):
         return [o for x, y, o in parts if x < b and a < y]
-    t16 = ew("t16", FL, NI, [lta], do=("t16",))
-    readers = {v: [] for v in range(RO)}
-    for b in range(1, NB):
-        readers[0] += start[b]
-    wrap, a32, bg, dl = {}, {}, {}, {}
-    sarr, tarr = {}, {}
-    first = [True]
 
-    def pieces(name, t, st, a, b, deps, win):
-        out = []
-        x = a
-        cut = c["CUT"].get(b - a) or [(c["PIECE"], FL)] * NI
-        while x < b:
-            y = min(b, x + cut[len(out)][0])
-            o = op("%s_%d" % (name, x), cut[len(out)][1], "gather", B * (y - x), deps + made[t], stage=(t, st), cols=(x, y), win=win)
-            readers[t].append(o)
-            out.append(o)
-            x = y
-        return out
+    def place(t, st):
+        return c["AT"].get(10 * t + st) or (c["ST"][st][0], c["ST"][st][1] + 10 * t, c["ST"][st][2])
 
-    def ext(name, t, st, a, b, gs, last=True):
-        return op(name, "E", "mm", B * max(64, b - a), gs + [dm], stage=(t, st), cols=(a, b), bank=name, do=("ext", last))
+    def chunks(t, st):
+        return FORM[place(t, st)[0]]
 
-    def sends(kind, t, split, srcs, via):
-        res = []
-        for a, b in ([(x, y) for x, y, _ in srcs] if split else [(0, NI)]):
-            o = op("send_%s%d_%d" % (kind, t, a), "P", "send", 0, over(srcs, a, b), via=via,
-                   do=("send", kind, t, a, b), sem="%s%d_%d" % (kind, t, a))
-            res.append((a, b, o))
-        return res
+    z2 = ew("zero_eye", "V", 128, [], do=("zero_eye",), pos=-9.0)
+    eye = ew("eye", "P", 256, [z2], do=("eye",), pos=-9.0)
+    io0 = ew("io0", "P", 12, [], do=("io0",), pos=-8.0)
+    io1 = ew("io1", "P", 12, [], do=("io1",), pos=-8.0)
+    z1 = ew("zero_dm", "V", 64, [], do=("zero_dm",), pos=-8.0)
+    io2 = ew("io2", "P", 16, [], do=("io2",), pos=-10.0)
+    ma = ew("ma", "V", 16, [io2], do=("ma",), pos=-9.0)
+    mb = ew("mb", "V", 16, [ma], do=("mb",), pos=-9.0)
+    dms = [ew("dm%d" % j, "APV"[j % 3], 64 if j % 3 == 2 else 128, [eye] if j % 3 == 1 else [eye, mb], do=("dm", j), pos=-4.0)
+           for j in range(B)]
+    dm = op("dm", "E", "mm", 0, dms + [z1], do=("none",))
+    ba = ew("ba", "V", 12, [io0], do=("ba",))
+    base = ew("base", "V", 24, [ba, io1], do=("base",))
+    eye32 = ew("eye32", "P", 256, [eye], do=("eye32",))
+    rot0 = ew("rot0", "P", 256, [eye], do=("rot0",))
+    rot = ew("rot", "P", 16, [rot0], do=("rot",))
+    one = ew("one", "V", 64, [], do=("one",))
+    kc = []
+    for rows, value in ((4, 2 * MID), (3, MID), (2, 0.25), (1, BIG)):
+        kc = [ew("kc%d" % rows, "V", 64, kc, do=("kc", rows, value))]
+    LD = [((x + H // 2) % H, (y + H // 2 - 1) % H + 1) for x, y in zip(c["LD"][:-1], c["LD"][1:])]
+    lds, un, chain, done = [], [], [], 0
+    for j, (x, y) in enumerate(LD):
+        done += 512 * (y - x)
+        lds.append(op("ld%d" % j, "S", "dma", done, [], do=("ld", x, y), sem="ld%d" % j))
+        chain.append(lds[-1])
+        if j == c["SA"]:
+            done += 512 * NI
+            lsa = op("ldsa", "S", "dma", done, [], do=("ldsa",), sem="ldsa")
+            chain.append(lsa)
+    lta = op("ldta", "S", "dma", done + 512 * NI, [], do=("ldta",), sem="ldta")
+    for x, y in zip(chain, chain[1:] + [lta]):
+        y["pre"] = x
+    for j, (x, y) in enumerate(LD):
+        un.append((x, y, ew("lo%d" % j, "V", y - x, [lds[j]], do=("lo", x, y), pos=-5.0)))
+        if j in c["AH"]:
+            h = ew("hj%d" % j, "A", y - x, [lds[j]], do=("hj", x, y), pos=-5.0)
+            un.append((H + x, H + y, ew("hk%d" % j, "A", y - x, [h], do=("hk", x, y), pos=-6.0)))
+        else:
+            un.append((H + x, H + y, ew("hi%d" % j, "V", y - x, [lds[j]], do=("hi", x, y), pos=-5.0)))
+    made = {0: [o for _, _, o in un]}
+    cp1 = [(x, y, ew("cp1_%d" % x, ("PA" if j < 8 else "VA")[j % 2], y - x, [o], do=("cp", 1, 0, x, y),
+                     pos=-0.4 + (x >= B * NI), row=j >= 8)) for j, (x, y, o) in enumerate(un)]
+    t16 = ew("t16", "A", NI, [lta], do=("t16",), pos=-0.3, row=True)
+    dl, sarr, tarr = {}, {}, {}
 
-    def remainder(nm, t, a, b, src, bank, buf, off, add, short):
-        if short:
-            i1 = ew(nm + "a", "V", b - a, [src], rb=bank, do=("quot", buf, t, a, b))
-            return ew(nm + "b", "V", b - a, [i1], rb=bank, do=("rem", buf, off, t, a, b))
-        i1 = ew(nm + "a", FL, b - a, [src], rb=bank, do=("conv", buf, t, a, b, add))
-        i2 = ew(nm + "b", "V", b - a, [i1], do=("and", buf, t, a, b))
-        return ew(nm + "c", "P" if "u" in c["pool"] else FL, b - a, [i2], do=("tou", buf, off, t, a, b))
+    def lookup(t, st, a, b, deps, win, opened=None):
+        form, at, gap = place(t, st)
+        pos = at + gap * FORM[form].index((a, b))
+        mid = a + 2 * int(round(c["SH"][st] * (b - a) / 2))
+        gs = [op("g%d%d_%d%s" % (t, st, x, q), q, "gather", B * (y - x), deps + made[t], stage=(t, st), cols=(x, y),
+                 win=win, pos=pos, row=True, reads=t) for x, y, q in ((a, mid, "A"), (mid, b, "V"))]
+        e = op("e%d%d_%d_%d" % (t, st, a, a), "E", "mm", B * max(64, b - a), gs + [dm] + ([opened] if opened else []),
+               stage=(t, st), cols=(a, b), do=("ext", opened is None), pos=pos - 100)
+        if opened is None:
+            e["bank"] = e["rb"] = e["name"]
+        else:
+            e["same"], e["rb"] = opened, opened["rb"]
+        return gs, e, e["rb"]
+
+    def sends(kind, t, srcs, via):
+        return [(a, b, op("send_%s%d_%d" % (kind, t, a), "P", "send", 0, [o], via=via,
+                          first=int(kind == "s" and t == 1 and a == srcs[0][0]), first2=int(via == "rel" and t == 1 and a == srcs[0][0]),
+                          pos="zsyt".index(kind) - 5.0, do=("send", kind, t, a, b), sem="%s%d_%d" % (kind, t, a))) for a, b, o in srcs]
+
+    def remainder(nm, t, a, b, src, bank, buf, off):
+        i1 = ew(nm + "a", ON["q" + buf[1]], b - a, [src], rb=bank, do=("conv", buf, t, a, b, -MID))
+        return ew(nm + "b", "V", b - a, [i1], rb=bank, do=("rem", buf, off, t, a, b))
 
     def bring(v):
-        b = v % NB
-        lo = max(0, v - NB)
-        prev = list(start[b]) if v < NB else readers[v - NB]
-        if copied(v):
-            lo = v - 1
-            pc = c["PC"]
+        x = v - 1
+        if v == 1:
+            cps, rest = over(cp1, 0, B * NI), over(cp1, B * NI, W)
+        else:
             cps = []
-            for x in range(0, B * NI, pc):
-                kw = dict(do=("cp", b, (v - 1) % NB, x, x + pc), late=prev)
-                if x < c["DC"]:
-                    cps.append(op("vc%d_%d" % (v, x), "S", "dma", 512 * pc, made[v - 1], sem="vc%d_%d" % (v, x), own=1, **kw))
+            for j, y in enumerate(range(0, B * NI, PIECE)):
+                kw = dict(do=("cp", v, x, y, y + PIECE), pos=10 * v - 15, reads=x)
+                if v > 2 and j % 3 == 2:
+                    cps.append(op("vc%d_%d" % (v, y), "S", "dma", 512 * PIECE, made[x][:1] + cps[-1:], sem="vc%d_%d" % (v, y), **kw))
                 else:
-                    cps.append(ew("vc%d_%d" % (v, x), c["VQ"], pc, made[v - 1], **kw))
-            readers[v - 1] += cps
-            prev = cps
-        if lo == v - 1 and NB > 1:
-            x = lo
-            cc = op("bcol%d" % x, FL, "gather", NI, [dl[x]] + made[x], do=("bcol", x, b), late=prev)
-            readers[x].append(cc)
-            made[v] = [op("scat%d_%d" % (x, v), "V", "scatter", NI, [dl[x], a32[x], cc], do=("scat", x, b))]
-            return
-        for x in range(lo, v):
-            if x not in bg:
-                bg[x] = op("bg%d" % x, FL, "gather", NI, [dl[x]] + made[x], do=("bg", x))
-                readers[x].append(bg[x])
-            sc = op("scat%d_%d" % (x, v), "V", "scatter", NI, [dl[x], a32[x]], do=("scat", x, b), late=prev)
-            cc = ew("col%d_%d" % (x, v), "P" if "c" in c["pool"] else FL, NI, [sc, bg[x]], do=("col", x, b))
-            prev = []
-            sc["deps"] += [] if x == lo else [last]
-            last = cc
-        made[v] = [last]
+                    cps.append(ew("vc%d_%d" % (v, y), "P", PIECE, made[x][:1], **kw))
+            if v > NB:
+                rest = []
+                for o in cps:
+                    o["deps"] += [u for u in ops if u.get("reads") == v - NB]
+            else:
+                src = over(cp1, B * NI, W) + made[max(1, v - 2)][:1]
+                rest = [op("tl%d" % v, "S", "dma", 512 * (W - B * NI), src, do=("cp", v, 1, B * NI, W), sem="tl%d" % v)]
+        cc = op("bcol%d" % x, ON["bcol"], "gather", NI, [dl[x]] + made[x][:1] + cps, do=("bcol", x), reads=x)
+        made[v] = [op("scat%d" % x, "V", "scatter", NI, [cc], do=("scat", x), reads=x)] + rest
 
     for t in range(RO):
         if t:
             bring(t)
-        wrap[t] = ew("wrap%d" % t, "P" if "w" in c["pool"] and t else FL, 1, made[t], do=("wrap", t % NB))
-        readers[t].append(wrap[t])
-        if t or RO > 1:
-            a32[t] = ew("a32_%d" % t, "P" if "a" in c["pool"] and t else FL, NI, made[t], do=("a32", t))
-            readers[t].append(a32[t])
+        wrap = ew("wrap%d" % t, "P", 1, made[t][:1] if t else over(un, 0, 1), do=("wrap", t), pos=1.0, reads=t)
         g1, c1u, c1h, c2, c3, c4, c5 = [], [], [], [], [], [], []
         for a, b in chunks(t, 1):
             nm = "%d_%d" % (t, a)
             if t == 0:
-                need = over(un, B * a, B * b)
-                i1 = ew("i1a" + nm, "V", 2 * (b - a), [lsa] + need, do=("sum0", a, b))
-                readers[0].append(i1)
-                i2 = ew("i1b" + nm, "V", b - a, [i1], do=("and", "m1", t, a, b))
-                i3 = ew("i1c" + nm, FL, b - a, [i2], do=("tou", "m1", "off1", t, a, b))
-            else:
-                ms = op("mms" + nm, "E", "mm", (5 + c["MS"]) * max(64, b - a), over(sarr[t], a, b) + [a32[t], eye, eye32, one, k2],
-                        bank="mms" + nm, do=("mms", t, a, b))
-                i3 = remainder("i1" + nm, t, a, b, ms, ms["bank"], "m1", "off1", MID, c["MS"])
-            gs = pieces("g1_%d" % t, t, 1, a, b, [i3], ("off1", W))
+                i1 = ew("i1a" + nm, "V", 2 * (b - a), [lsa] + over(un, B * a, B * b), do=("sum0", a, b), pos=-5.5 + 100 * bool(g1))
+                i2 = ew("i1b" + nm, "V", b - a, [i1], do=("and", a, b), pos=-5.6 + 100 * bool(g1))
+                i3 = ew("i1c" + nm, "A", b - a, [i2], do=("tou", a, b), pos=-7.0)
+            elif not g1:
+                ms = op("mms" + nm, "E", "mm", 6 * NI, over(sarr[t], 0, NI) + made[t][:1] + [eye, eye32, one] + kc,
+                        bank="mms" + nm, rb="mms" + nm, do=("mms", t, 0, NI), pos=-300.0, reads=t)
+                i3 = remainder("i1" + nm, t, 0, NI, ms, ms["bank"], "m1", "off1")
+            gs, e, bank = lookup(t, 1, a, b, [i3], ("off1", W))
             g1 += gs
-            e = ext("e1" + nm, t, 1, a, b, gs)
-            if t < RO - 1:
-                h = ew("c1h" + nm, FL, b - a, [e], rb=e["bank"], do=("conv", "so", t, a, b, 0.0))
-            else:
-                h = ew("c1h" + nm, FL, b - a, [e], rb=e["bank"], do=("conv", "oys", 0, a, b, MID))
-            u = ew("c1u" + nm, FL, b - a, [e], rb=e["bank"], do=("conv", "off2", t, a, b, MID))
-            c1u.append((a, b, u)); c1h.append((a, b, h))
-        if t < RO - 1:
-            sarr[t + 1] = sends("s", t + 1, c["SS"], c1h, "rel")
-            dmm = op("dmm%d" % t, "E", "mm", B * 64, g1 + [dm], stage=(t, 1), bank="dmm%d" % t, do=("dmm",))
-            d1 = ew("d1_%d" % t, FL, 12, [dmm], rb=dmm["bank"], do=("d1", t))
+            c1u.append((a, b, ew("c1u" + nm, ON["c1u"], b - a, [e], rb=bank, do=("conv", "off2", t, a, b, MID), pos=-2.0)))
+            if t == 0:
+                c1h.append((a, b, ew("c1h" + nm, ON["c1h"], b - a, [e], rb=bank, do=("conv", "so", t, a, b, 0.0), pos=-3.0)))
+        if t == RO - 1:
+            c1h = [(0, NI, ew("c1h%d" % t, "V", NI, over(c1u, 0, NI), do=("half", "oys", t, 0, NI, 0.0), pos=99.0))]
+            op("stys", "S", "dma", 512 * NI, over(c1h, 0, NI), do=("st", "ys", 0, NI), sem="stys")
+        else:
+            if t:
+                c1h = [(0, NI, ew("c1h%d" % t, "V", NI // 2, over(c1u, 0, NI), do=("half", "so", t, 0, NI, -MID), pos=-3.0))]
+            sarr[t + 1] = sends("s", t + 1, c1h, "rel")
+            dmm = op("dmm%d" % t, "E", "mm", B * 64, g1 + [dm], stage=(t, 1), bank="dmm%d" % t, rb="dmm%d" % t, do=("dmm",), pos=-200.0)
+            d1 = ew("d1_%d" % t, ON["d1"], 12, [dmm], rb=dmm["bank"], do=("d1", t))
             d2 = ew("d2_%d" % t, "V", 12, [d1], do=("d2", t))
             dl[t] = ew("d3_%d" % t, "V", 24, [d2, base], do=("d3", t))
-        else:
-            op("stys", "S", "dma", 98304, over(c1h, 0, NI), do=("st", "ys", 0, NI), sem="stys")
         for a, b in chunks(t, 2):
-            nm = "%d_%d" % (t, a)
-            e = ext("e2" + nm, t, 2, a, b, pieces("g2_%d" % t, t, 2, a, b, over(c1u, a, b), ("off2", W)))
-            c2.append((a, b, ew("c2" + nm, FL, b - a, [e], rb=e["bank"], do=("conv", "zout", t, a, b, MID))))
-        za = sends("z", t, c["ZS"], c2, "hop")
+            gs, e, bank = lookup(t, 2, a, b, over(c1u, a, b), ("off2", W))
+            c2.append((a, b, ew("c2%d_%d" % (t, a), ON["c2"], b - a, [e], rb=bank, do=("conv", "zout", t, a, b, MID))))
+        za = sends("z", t, c2, "hop")
         for a, b in chunks(t, 3):
-            nm = "%d_%d" % (t, a)
-            e = ext("e3" + nm, t, 3, a, b, pieces("g3_%d" % t, t, 3, a, b, over(za, a, b), ("zin", W)))
-            c3.append((a, b, ew("c3" + nm, FL, b - a, [e], rb=e["bank"], do=("conv", "zret", t, a, b, MID + 1))))
-        zb = sends("y", t, c["ZS"], c3, "hop")
+            gs, e, bank = lookup(t, 3, a, b, over(za, a, b), ("zin", W))
+            c3.append((a, b, ew("c3%d_%d" % (t, a), ON["c3"], b - a, [e], rb=bank, do=("conv", "zret", t, a, b, MID + 1))))
+        zb = sends("y", t, c3, "hop")
         for a, b in chunks(t, 4):
             nm = "%d_%d" % (t, a)
             src = over(tarr[t], a, b) if t else [t16]
-            e = ext("e4" + nm, t, 4, a, b, pieces("g4_%d" % t, t, 4, a, b, over(zb, a, b) + [wrap[t]], ("zback", W + 1)), last=False)
-            e["pre"] += src
-            mt = op("mmt" + nm, "E", "mm", (1 + c["MT"]) * max(64, b - a), src + [rot, one, k1, e], same=e, rb=e["bank"], do=("mmt", t, a, b))
-            c4.append((a, b, remainder("i5" + nm, t, a, b, mt, e["bank"], "m5", "off5", 3 * MID, c["MT"])))
+            mk = op("mmk" + nm, "E", "mm", max(64, b - a), [one] + kc, bank="mmk" + nm, rb="mmk" + nm, do=("mmk", a, b), pos=-400.0)
+            gs, e, bank = lookup(t, 4, a, b, over(zb, a, b) + [wrap], ("zback", W + 1), mk)
+            mk["deps"] = gs[:1] + mk["deps"]
+            mt = op("mmt" + nm, "E", "mm", max(64, b - a), src + [rot, e], same=e, rb=bank, do=("mmt", t, a, b), pos=-300.0)
+            c4.append((a, b, remainder("i5" + nm, t, a, b, mt, bank, "m5", "off5")))
         for a, b in chunks(t, 5):
             nm = "%d_%d" % (t, a)
-            e = ext("e5" + nm, t, 5, a, b, pieces("g5_%d" % t, t, 5, a, b, over(c4, a, b), ("off5", W)))
+            gs, e, bank = lookup(t, 5, a, b, over(c4, a, b), ("off5", W))
             if t < RO - 1:
-                c5.append((a, b, ew("c5" + nm, FL, b - a, [e], rb=e["bank"], do=("conv", "to", t, a, b, 0.0))))
+                c5.append((a, b, ew("c5" + nm, ON["c5"], b - a, [e], rb=bank, do=("conv", "to", t, a, b, 0.0))))
             else:
-                x = ew("c5" + nm, FL, b - a, [e], rb=e["bank"], do=("conv", "oyt", 0, a, b, MID))
+                x = ew("c5" + nm, ON["c5"], b - a, [e], rb=bank, do=("conv", "oyt", 0, a, b, MID))
                 op("styt%d" % a, "S", "dma", 512 * (b - a), [x], do=("st", "yt", a, b), sem="styt%d" % a)
         if t < RO - 1:
-            tarr[t + 1] = sends("t", t + 1, c["TS"], c5, "rel")
+            tarr[t + 1] = sends("t", t + 1, c5, "rel")
     for o in ops:
-        o["deps"] = o["deps"] + list(o.get("late", []))
+        nm = o["name"]
+        key = None
+        if nm[:3] in ("c1u", "c1h") or nm[:2] in ("c2", "c3", "c5"):
+            x = 3 if nm[:2] == "c1" else 2
+            t, key = int(nm[x]), nm[:x] + "ab"[nm[x + 2:] not in ("0", "")]
+        elif nm[:2] in ("i1", "i5") and nm[2].isdigit():
+            t, key = int(nm[2]), "qr"[nm[-1] == "b"] + nm[1] + "ab"[nm[4:-1] != "0"]
+        elif nm[:2] in ("d1", "d2", "d3") or nm[:4] in ("bcol", "scat"):
+            t, key = int(nm[-1]), nm[:2] if nm[0] == "d" else nm[:4]
+        if key in c["PAT"] and 1 <= t + (key[1] == "5") <= 4:
+            q, at = c["PAT"][key]
+            o["q"], o["pos"], o["row"] = q, 10 * t + at + 0.0001 * o["i"] / len(ops), True
+    for q in "AV":
+        row = sorted((o for o in ops if o["q"] == q and o.get("row")), key=lambda o: o["pos"])
+        for x, y in zip(row, row[1:]):
+            y["pre"] = x
     return ops
 
 
 def schedule(c):
     ops = build(c)
-    m = nominal(c)
-    rs = np.random.RandomState(c["seed"])
     users = [[] for _ in ops]
+    use = {}
     for o in ops:
+        o["t1"] = None
         for d in o["deps"]:
             users[d["i"]].append(o)
-    order, left = [], [len(o["deps"]) for o in ops]
-    todo = [o for o in ops if not o["deps"]]
-    while todo:
-        o = todo.pop()
-        order.append(o)
-        for u in users[o["i"]]:
-            left[u["i"]] -= 1
-            if not left[u["i"]]:
-                todo.append(u)
-    for o in reversed(order):
-        o["pr"] = cost(o, o["q"][0], m)[1] + max([u["pr"] for u in users[o["i"]]] + [0.0])
-    for o in ops:
-        o["pr"] += c["jit"] * float(rs.rand())
-        if o["k"] == "gather" and "stage" in o:
-            o["pr"] += c["BIAS"][5 * o["stage"][0] + o["stage"][1] - 1] - c["slope"] * o["cols"][0] / NI
-        elif o.get("do", ("",))[0] != "cp":
-            o["pr"] += c["sb"]
-    if c["PRI"]:
-        for o in ops:
-            o["pr"] = -c["PRI"][o["i"]]
-            o["q"] = c["ON"][o["i"]] if c["ON"] else o["q"]
-    guse, buse = {}, {}
-    for o in ops:
-        if "stage" in o:
-            guse.setdefault(o["stage"], []).append(o)
-        for key in ("bank", "rb"):
+        for key in ("stage", "rb"):
             if key in o:
-                buse.setdefault(o[key], []).append(o)
-    gslot, bslot = {}, {}
-    gown, bown = [None] * c["NG"], [None] * 8
+                use.setdefault(o[key], []).append(o)
+    slot = {}
+    own = {"stage": [[] for _ in range(NG)], "rb": [[] for _ in range(8)]}
     free = {q: 0.0 for q in "AVPES"}
     left = [len(o["deps"]) for o in ops]
-    ready = [o for o in ops if not o["deps"]]
-    done = []
+    ready, done = [], []
 
-    def pick(own, use):
-        best = None
-        for s, w in enumerate(own):
-            us = [] if w is None else use[w]
-            if all("t1" in u for u in us):
-                tt = max([u["t1"] for u in us] + [0.0])
-                if best is None or tt < best[0]:
-                    best = (tt, s, us)
-        return best
+    def arrive(o):
+        o["r"] = max([(d["te"] if d is o.get("same") else d["t1"]) for d in o["deps"]] + [0.0])
+        ready.append(o)
 
     def earliest(o):
-        if any("t1" not in p for p in o["pre"]):
-            return None
-        r = max([(d["te"] if d is o.get("same") else d["t1"]) for d in o["deps"]] + [0.0])
         extra, take = [], None
-        if o["k"] == "gather" and "stage" in o:
-            if o["stage"] not in gslot:
-                p = pick(gown, guse)
-                if p is None:
-                    return None
-                take = ("g", p[1]); extra = [u for u in p[2] if u["k"] == "mm"]
-            else:
-                extra = gslot[o["stage"]][1]
-        if "bank" in o:
-            p = pick(bown, buse)
-            if p is None:
+        key = "rb" if "bank" in o else "stage" if o["k"] == "gather" and "stage" in o else None
+        if key and o[key] not in slot:
+            can = [(max([u["t1"] for u in us] + [0.0]), s) for s, us in enumerate(own[key]) if all(u["t1"] is not None for u in us)]
+            if not can:
                 return None
-            take = ("b", p[1]); extra = p[2]
-        if "rb" in o and "same" not in o:
-            extra = [u for u in buse[o["rb"]] if "t1" in u]
-        r = max([r] + [u["t1"] for u in extra])
-        return r, extra, take
+            take = (key, min(can)[1])
+            extra = [u for u in own[key][take[1]] if u["k"] != "gather"]
+        elif key:
+            extra = slot[o[key]][1]
+        elif "rb" in o and "same" not in o:
+            extra = [u for u in use[o["rb"]] if u["t1"] is not None and u["q"] != o["q"]]
+        return max([o["r"]] + [u["t1"] for u in extra]), extra, take
 
+    for o in ops:
+        if not o["deps"]:
+            arrive(o)
     while ready:
         cand = []
         for o in ready:
-            e = earliest(o)
-            if e is not None:
-                for q in o["q"]:
-                    cand.append((max(e[0], free[q]), q, o, e))
-        t0, q0 = min((x[0], x[1]) for x in cand)
-        _, q, o, e = max((x for x in cand if x[1] == q0 and x[0] <= t0 + c["look"]), key=lambda x: (x[2]["pr"], -x[2]["i"]))
-        o["on"] = q
-        if o["k"] == "send":
-            o["first"] = int(not any(x["k"] == "send" for x in done))
-            o["first2"] = int(o["via"] == "rel" and not any(x.get("via") == "rel" for x in done))
-        o["t0"] = max(e[0], free[q])
-        hold, fin = cost(o, q, m)
-        o["te"], o["t1"] = o["t0"] + hold, o["t0"] + fin
+            if o["pre"] is None or o["pre"]["t1"] is not None:
+                e = earliest(o)
+                if e is not None:
+                    cand += [(max(e[0], free[q]), q, o, e) for q in o["q"]]
+        t0, q = min((x[0], x[1]) for x in cand)
+        look = c["lookp"] if q == "P" else 0.0
+        s, q, o, e = min((x for x in cand if x[1] == q and x[0] <= t0 + c["wait"].get(x[2].get("do", "g")[0], look)),
+                         key=lambda x: (x[2]["pos"], x[2]["i"]))
+        o["q"], o["t0"] = q, s
+        hold, fin = cost(o, c)
+        o["te"], o["t1"] = s + hold, s + fin
         free[q] = o["te"]
         o["deps"] = o["deps"] + [u for u in e[1] if all(u is not d for d in o["deps"])]
         if e[2] is not None:
-            if e[2][0] == "g":
-                gown[e[2][1]] = o["stage"]; gslot[o["stage"]] = (e[2][1], e[1])
-            else:
-                bown[e[2][1]] = o["bank"]; bslot[o["bank"]] = e[2][1]
-        ready = [x for x in ready if x is not o]
+            key, x = e[2]
+            own[key][x] = use[o[key]]
+            slot[o[key]] = (x, e[1])
+        ready.remove(o)
         done.append(o)
         for u in users[o["i"]]:
             left[u["i"]] -= 1
             if not left[u["i"]]:
-                ready.append(u)
+                arrive(u)
     for o in done:
         if "stage" in o:
-            o["g"] = gslot[o["stage"]][0]
-        for key in ("bank", "rb"):
-            if key in o:
-                o["ps"] = bslot[o[key]]
-    last, into, out = {}, {}, []
+            o["g"] = slot[o["stage"]][0]
+        if "rb" in o:
+            o["ps"] = slot[o["rb"]][0]
     done.sort(key=lambda x: x["t0"])
-    for o in done:
-        p = last.get(o["on"])
-        if (p is not None and o["k"] == "gather" and p["k"] == "gather" and "stage" in o and o.get("stage") == p.get("stage")
-                and p["cols"][1] == o["cols"][0] and all(d["t1"] <= p["t0"] + 1e-9 for d in o["deps"])
-                and p["n"] + o["n"] <= B * c.get("MAXP", 96)):
-            p["cols"] = (p["cols"][0], o["cols"][1]); p["n"] += o["n"]
-            p["deps"] = p["deps"] + [d for d in o["deps"] if all(d is not x for x in p["deps"])]
-            into[o["i"]] = p
-            continue
-        last[o["on"]] = o
-        out.append(o)
-    for o in out:
-        ds = []
-        for d in o["deps"]:
-            d = into.get(d["i"], d)
-            if all(d is not x for x in ds):
-                ds.append(d)
-        o["deps"] = ds
-    return out
-
-
-def timing(plan, m):
-    free = {q: 0.0 for q in "AVPES"}
-    te, t1, busy = {}, {}, []
-    for o in plan:
-        s = max([free[o["on"]]] + [(te if d is o.get("same") else t1)[d["i"]] for d in o["deps"]])
-        hold, fin = cost(o, o["on"], m)
-        if o.get("own"):
-            busy.append((s, s + hold))
-        if o["k"] == "send":
-            fin += max([y - s - hold for x, y in busy if x < s + hold < y] + [0.0])
-        te[o["i"]], t1[o["i"]] = s + hold, s + fin
-        free[o["on"]] = s + hold
-    return max(t1.values())
+    return done
 
 
 PLAN = schedule(CFG)
@@ -416,15 +330,16 @@ SEMAPHORES = ["qA", "qV", "qP", "qE", "left"] + [o["sem"] for o in PLAN if "sem"
 LAND = {"z": ("zout", "zin"), "y": ("zret", "zback"), "s": ("so", "si"), "t": ("to", "ti")}
 
 
-def low_engines(topo, src, dst):
-    m = topo.mask(src, dst)
-    return m, len(topo.engines(src, dst))
-
-
-def relay_of(topo, T, src, dst):
+def relay_of(topo, T, src, dst, kind):
     if topo.may_write(src, dst):
         return None
-    return [x for x in topo.cores_of(src) if T.rank_of(x) is None and topo.die(x) == topo.die(src) and topo.may_write(x, dst)][0]
+    can = [x for x in topo.cores_of(src) if T.rank_of(x) is None and topo.die(x) == topo.die(src) and topo.may_write(x, dst)]
+    return can[0] if kind == "s" else can[-1]
+
+
+def engines_of(topo, o, src, dst, far):
+    e = topo.engines(src, far if o["do"][1:3] == ("s", 1) else dst)
+    return sum(1 << x for x in e), len(e)
 
 
 def rank_program(g, core, T, topo):
@@ -434,54 +349,71 @@ def rank_program(g, core, T, topo):
     if rank is None:
         for r in range(N):
             src, dst = T.cores[r], T.cores[(r + 1) % N]
-            if relay_of(topo, T, src, dst) == core:
-                mask, ne = low_engines(topo, core, dst)
-                nin = low_engines(topo, src, T.cores[(r + DQ) % N])[1]
+            mine = [kind for kind in "st" if relay_of(topo, T, src, dst, kind) == core]
+            if mine:
+                mask, ne = topo.mask(core, dst), len(topo.engines(core, dst))
                 rid, pid = topo.addr(dst, core)
                 tot = 0
                 for o in PLAN:
-                    if o["k"] == "send" and o["via"] == "rel":
+                    if o["k"] == "send" and o["do"][1] in mine:
                         _, kind, t, a, b = o["do"]
                         ap = T[LAND[kind][1]][:, t * NI + a:t * NI + b]
-                        g.wait_ge(S[o["sem"]], nin)
+                        g.wait_ge(S[o["sem"]], engines_of(topo, o, src, core, T.cores[(r + DQ) % N])[1])
                         g.remote_dma(ap, ap, S[o["sem"]], S.left, pid, rid, mask)
                         tot += ne
                 g.wait_ge(S.left, tot)
         return
     nxt, prv, par = T.cores[(rank + 1) % N], T.cores[(rank - 1) % N], T.cores[(rank + DQ) % N]
-    mask, ne = low_engines(topo, core, par)
-    rel = relay_of(topo, T, core, nxt)
-    rin = relay_of(topo, T, prv, core)
-    to = {"hop": par, "rel": nxt if rel is None else rel}
-    gain = {"hop": low_engines(topo, par, core)[1], "rel": low_engines(topo, prv if rin is None else rin, core)[1]}
+    to = {"z": par, "y": par}
+    gain = {"z": len(topo.engines(par, core)), "y": len(topo.engines(par, core))}
+    for kind in "st":
+        rel, rin = relay_of(topo, T, core, nxt, kind), relay_of(topo, T, prv, core, kind)
+        to[kind] = nxt if rel is None else rel
+        gain[kind] = len(topo.engines(prv if rin is None else rin, core))
     Q = {"A": g.scalar, "V": g.vector, "P": g, "E": g.tensor, "S": g.sync}
     V, PE = g.vector, g.tensor
-    NB = CFG["NB"]
 
     def sl(name, t, a, b):
+        t = t if T[name].shape[1] > NI else 0
         return T[name][:, t * NI + a:t * NI + b]
+
+    def tb(v):
+        return T["tb%d" % (v if v <= NB else v - NB)]
 
     def affine(q, out, in_, add):
         if q == "A":
             return g.scalar.activation(out, in_, AF.Identity, bias=float(add)) if add else g.scalar.activation(out, in_, AF.Copy)
         if q == "P":
             return g.affine_select(out, in_, [[0, int(out.shape[1])]], AL.is_ge, 0.0, 0, 0)
+        if q == "S":
+            return g.sync.dma_start(out, in_)
         return V.tensor_scalar(out, in_, float(add), None, AL.add) if add else V.tensor_copy(out, in_)
 
     def emit(o):
-        q = o["on"]
+        q = o["q"]
         if o["k"] == "gather" and "stage" in o:
             t, (a, b), (off, w) = o["stage"][0], o["cols"], o["win"]
-            return affine(q, T["gb%d" % o["g"]][:, B * a:B * b], T["tb%d" % (t % NB)][:, 0:w].indirect(sl(off, t, a, b)), -MID)
+            return affine(q, T["gb%d" % o["g"]][:, B * a:B * b], tb(t)[:, 0:w].indirect(sl(off, t, a, b)), -MID)
         d = o["do"]
         k = d[0]
         ps = T["ps%d" % o["ps"]] if "ps" in o else None
         if k == "zero_dm":
-            return V.memset(T.dm[:], 0.0)
+            return V.memset(T.dm[:, 0:16], 0.0)
         if k == "zero_eye":
             return V.memset(T.eye2[:], 0.0)
         if k == "dm":
-            return g.affine_select(T.dm[:, 16:], T.dm[:, 16:], [[-1024, 16], [-16, 8], [1023, 16]], AL.not_equal, 1.0, 0, 1)
+            out, col = T.dm[:, 16 + 128 * d[1]:144 + 128 * d[1]], T.mk[:, d[1]:d[1] + 1]
+            if q == "A":
+                return g.scalar.activation(out, T.eye2[:, 0:128], AF.Identity, scale=col)
+            if q == "P":
+                return g.affine_select(out, T.eye2[:, 0:128], [[0, 8], [1, B]], AL.is_equal, 0.0, -d[1], 0)
+            return V.tensor_scalar(out, T.eye2[:, 0:128], col, None, AL.mult)
+        if k == "io2":
+            return g.iota(T.mi[:], [[-1, B]], B, 1)
+        if k == "ma":
+            return V.tensor_scalar(T.mi[:], T.mi[:], B - 1, None, AL.bitwise_and)
+        if k == "mb":
+            return V.tensor_scalar(T.mk[:], T.mi[:], 0.0, None, AL.is_equal)
         if k == "io0":
             return g.iota(T.b0[:], [[0, 12]], 0, B)
         if k == "io1":
@@ -493,7 +425,7 @@ def rank_program(g, core, T, topo):
         if k == "eye":
             return g.affine_select(T.eye2[:], T.eye2[:], [[0, 2], [-1, 128]], AL.not_equal, 1.0, 0, 1)
         if k == "eye32":
-            return affine("P", T.eye32[:], T.eye2[:, 0:128], 0)
+            return affine("P", T.eye32[:], T.eye2[:], 0)
         if k == "rot0":
             return g.affine_select(T.rot2[:], T.eye2[:], [[0, 2], [-1, 128]], AL.not_equal, 1.0, -1, 1)
         if k == "rot":
@@ -515,81 +447,65 @@ def rank_program(g, core, T, topo):
                                        bias=2.0 ** -13 + 0.5 - MID, scale=1.0 / W)
         if k == "hk":
             return affine(q, T.tb0[:, H + d[1]:H + d[2]], T.tb0[:, H + d[1]:H + d[2]], MID - 1)
-        if k == "cp" and q == "S":
-            return g.sync.dma_start(T["tb%d" % d[1]][:, d[3]:d[4]], T["tb%d" % d[2]][:, d[3]:d[4]])
         if k == "cp":
-            return affine(q, T["tb%d" % d[1]][:, d[3]:d[4]], T["tb%d" % d[2]][:, d[3]:d[4]], 0)
+            return affine(q, tb(d[1])[:, d[3]:d[4]], tb(d[2])[:, d[3]:d[4]], 0)
         if k == "one":
-            return V.memset(T.one[0:2, :], 1.0)
-        if k == "k0":
-            return V.memset(T.kt[0:2, :], 0.25)
-        if k == "k1":
-            return V.memset(T.kt[0:1, :], 3 * MID + W)
-        if k == "k2":
-            return V.memset(T.ks[0:1, :], MID)
-        if k == "quot":
-            _, name, t, a, b = d
-            if name == "m1":
-                return V.tensor_scalar(sl(name, t, a, b), ps[:, 0:b - a], float(W), float(W), AL.is_ge, AL.mult)
-            return V.tensor_scalar(sl(name, t, a, b), ps[:, 0:b - a], 2.0 ** 35 - MID, 2.0 ** 35, AL.add, AL.subtract)
+            return V.memset(T.one[0:4, :], 1.0)
+        if k == "kc":
+            return V.memset(T.kc[0:d[1], :], d[2])
         if k == "rem":
             _, name, off, t, a, b = d
             return V.tensor_tensor(sl(off, t, a, b), ps[:, 0:b - a], sl(name, t, a, b), AL.subtract)
         if k == "t16":
             return affine(q, sl("ti", 0, 0, NI), T.tab[:], -MID)
         if k == "wrap":
-            tb = T["tb%d" % d[1]]
-            return affine(q, tb[:, W:W + 1], tb[:, 0:1], 0)
-        if k == "a32":
-            return affine(q, sl("a32", d[1], 0, NI), T["tb%d" % (d[1] % NB)][:, d[1]:B * NI:B], 0)
+            return affine(q, tb(d[1])[:, W:W + 1], tb(d[1])[:, 0:1], 0)
         if k == "sum0":
-            return V.tensor_tensor(sl("m1", 0, d[1], d[2]), T.sab[:, d[1]:d[2]], T.tb0[:, B * d[1]:B * d[2]:B], AL.add)
+            return V.tensor_tensor(T.m0[:, d[1]:d[2]], T.sab[:, d[1]:d[2]], T.tb0[:, B * d[1]:B * d[2]:B], AL.add)
+        if k == "and":
+            return V.tensor_scalar(T.m0[:, d[1]:d[2]], T.m0[:, d[1]:d[2]], W - 1, None, AL.bitwise_and)
+        if k == "tou":
+            return affine(q, T.off1[:, d[1]:d[2]], T.m0[:, d[1]:d[2]], 0)
         if k == "mms":
             _, t, a, b = d
             PE.matmul(ps[:, 0:b - a], T.eye2[:, 128 - B * GS:256 - B * GS], sl("si", t, a, b), True, False)
-            if CFG["MS"]:
-                PE.matmul(ps[:, 0:b - a], T.one[0:1, :], T.ks[0:1, 0:b - a], False, False)
-            return PE.matmul(ps[:, 0:b - a], T.eye32[:], sl("a32", t, a, b), False, True)
+            PE.matmul(ps[:, 0:b - a], T.one[0:3, :], T.kc[0:3, 0:b - a], False, False)
+            return PE.matmul(ps[:, 0:b - a], T.eye32[:, 0:128], tb(t)[:, B * a + t:B * b:B], False, True)
+        if k == "mmk":
+            return PE.matmul(ps[:, 0:d[2] - d[1]], T.one[0:4, :], T.kc[0:4, 0:d[2] - d[1]], True, False)
         if k == "mmt":
             _, t, a, b = d
             x = 128 - B * GS if t else 0
-            if CFG["MT"]:
-                PE.matmul(ps[:, 0:b - a], T.one[0:2, :], T.kt[0:2, 0:b - a], False, False)
             return PE.matmul(ps[:, 0:b - a], T.rot2[:, x:x + 128], sl("ti", t, a, b), False, True)
         if k == "ext":
             a, b = o["cols"]
             for j in range(B):
                 r = PE.matmul(ps[:, 0:b - a], T.dm[:, 16 + 128 * j:144 + 128 * j], T["gb%d" % o["g"]][:, B * a + j:B * b:B],
-                              j == 0, d[1] and j == B - 1)
+                              d[1] and j == 0, d[1] and j == B - 1)
             return r
         if k == "dmm":
             for j in range(B):
                 r = PE.matmul(ps[:, 0:12], T.dm[:, 16 - j:144 - j], T["gb%d" % o["g"]][:, B * j:B * NI:B * B], j == 0, j == B - 1)
             return r
-        if k == "toint" or k == "conv":
+        if k == "conv":
             _, name, t, a, b, add = d
             return affine(q, sl(name, t, a, b), ps[:, 0:b - a], add)
-        if k == "and":
-            ap = sl(d[1], d[2], d[3], d[4])
-            return V.tensor_scalar(ap, ap, W - 1, None, AL.bitwise_and)
-        if k == "tou":
-            return affine(q, sl(d[2], d[3], d[4], d[5]), sl(d[1], d[3], d[4], d[5]), 0)
+        if k == "half":
+            _, name, t, a, b, add = d
+            return affine(q, sl(name, t, a, b), sl("off2", t, a, b), add)
         t = d[1]
+        lst = T.dl[:, 16 * t:16 * t + 12]
         if k == "d1":
             return affine(q, T.dt[:, 16 * t:16 * t + 12], ps[:, 0:12], MID)
         if k == "d2":
             ap = T.dt[:, 16 * t:16 * t + 12]
             return V.tensor_scalar(ap, ap, B - 1, None, AL.bitwise_and)
         if k == "d3":
-            return V.tensor_tensor(T.dl[:, 16 * t:16 * t + 12], T.dt[:, 16 * t:16 * t + 12], T.base[:], AL.add)
-        if k == "bg":
-            return affine(q, sl("b32", t, 0, NI), T["tb%d" % (t % NB)][:, 0:W].indirect(T.dl[:, 16 * t:16 * t + 12]), 0)
+            return V.tensor_tensor(lst, T.dt[:, 16 * t:16 * t + 12], T.base[:], AL.add)
         if k == "bcol":
-            return affine(q, T["tb%d" % d[2]][:, t:B * NI:B], T["tb%d" % (t % NB)][:, 0:W].indirect(T.dl[:, 16 * t:16 * t + 12]), 0)
+            return affine(q, tb(t + 1)[:, t:B * NI:B], tb(t)[:, 0:B * NI].indirect(lst), 0)
         if k == "scat":
-            return V.tensor_copy(T["tb%d" % d[2]][:, 0:W].indirect(T.dl[:, 16 * t:16 * t + 12]), sl("a32", t, 0, NI))
-        if k == "col":
-            return affine(q, T["tb%d" % d[2]][:, t:B * NI:B], sl("b32", t, 0, NI), 0)
+            return V.tensor_copy(tb(t + 1)[:, 0:B * NI].indirect(lst), tb(t)[:, t:B * NI:B])
         raise ValueError(k)
 
     count = {q: 0 for q in "AVPE"}
@@ -608,17 +524,20 @@ def rank_program(g, core, T, topo):
                     known[q][n2] = v2
 
     for o in PLAN:
-        q = o["on"]
+        q = o["q"]
         for d in sorted(o["deps"], key=lambda x: -x["t1"]):
-            if d is not o.get("same"):
+            if d is not o.get("same") and mark[d["i"]]:
                 wait(q, mark[d["i"]][0], mark[d["i"]][1], clock[d["i"]])
-        if o["k"] == "send":
+        if o.get("do") == ("none",):
+            mark[o["i"]] = None
+        elif o["k"] == "send":
             _, kind, t, a, b = o["do"]
             ts = t - 1 if o["via"] == "rel" else t
-            rid, pid = topo.addr(to[o["via"]], core)
+            rid, pid = topo.addr(to[kind], core)
+            mask, ne = engines_of(topo, o, core, to[kind], par)
             g.remote_dma(sl(LAND[kind][1], t, a, b), sl(LAND[kind][0], ts, a, b), S[o["sem"]], S.left, pid, rid, mask)
             sent += ne
-            mark[o["i"]], clock[o["i"]] = (o["sem"], gain[o["via"]]), {}
+            mark[o["i"]], clock[o["i"]] = (o["sem"], gain[kind]), {}
         elif o["k"] == "dma":
             emit(o).then_inc(S[o["sem"]], 16)
             mark[o["i"]], clock[o["i"]] = (o["sem"], 16), dict(known[q])

from concourse.mybir import AluOpType as AL, ActivationFunctionType as AF

W, H, B, NI, RO, GS, DQ = 4096, 2048, 16, 192, 6, 5, 3
MID = 2048.0
BIG = 1.5 * 2.0 ** 19
NB, NG, PIECE = 4, 8, 512
FORM = {"2": [(0, 96), (96, 192)], "3": [(0, 64), (64, 128), (128, 192)], "m": [(64, 128), (0, 64), (128, 192)]}
CFG = dict(
    LD=[0, 256, 512, 1024, 1408, 1792, 2048], SA=2, AH=[0, 2],
    ST={1: ("2", 0, 1), 2: ("2", 2, 2), 3: ("2", 7, 2), 4: ("2", 13, 2), 5: ("2", 16, 2)},
    SH={1: 0.52, 2: 0.54, 3: 0.52, 4: 0.5, 5: 0.54},
    AT={1: ("m", -17.0, 0.25), 2: ("2", -9.5, 1.5), 3: ("2", 6.5, 1.5), 51: ("2", 49.5, 0.25), 52: ("2", 52.0, 3.0),
        44: ("2", 55.0, 0.25), 53: ("3", 55.5, 2.0), 45: ("3", 57.0, 2.0), 54: ("3", 63.0, 1.5), 55: ("3", 70.0, 1.5)},
    PAT=dict(q1a=("A", -2.45), r1a=("V", -1.4), c1ua=("V", 1.6), d1=("A", 2.65), c1ub=("A", 2.8), c1ha=("V", 3.5),
             d2=("V", 3.51), d3=("V", 4.65), bcol=("A", 4.65), c2a=("V", 4.75), c2b=("A", 5.5), scat=("V", 5.55),
             c3a=("V", 9.55), c3b=("V", 11.8), q5a=("A", 14.75), r5a=("V", 15.5), q5b=("V", 16.55), r5b=("V", 16.8),
             c5a=("V", 18.55), c5b=("A", 21.7)),
    ON=dict(c1h="V", c1u="V", c2="V", c3="V", c5="AV", q1="A", q5="V", d1="V", bcol="A"),
    wait=dict(cp=0.06, d1=0.8, send=0.8, bcol=0.2, conv=0.06, d2=0.2, half=0.5), lookp=0.05,
    f=1.15, cg=1.5, cs=3.8, pe=0.45, wake=0.12, iss=0.3, hop=1.5, rel=3.0, first=0.8, dma0=1.6, bw=250.0)

SCRATCH = {
    "one": ("sbuf", [128, 128], "bfloat16"), "kc": ("sbuf", [128, NI], "bfloat16"), "m0": ("sbuf", [128, NI], "int32"),
    "pmb": ("sbuf", [128, H], "int32"), "sab": ("sbuf", [128, NI], "int32"), "tab": ("sbuf", [128, NI], "int32"),
    "dm": ("sbuf", [128, 16 + 2048], "bfloat16"), "eye2": ("sbuf", [128, 256], "bfloat16"),
    "rot2": ("sbuf", [128, 256], "bfloat16"), "eye32": ("sbuf", [128, 256], "float32"),
    "mi": ("sbuf", [128, B], "int32"), "mk": ("sbuf", [128, B], "float32"),
    "b0": ("sbuf", [128, 12], "int32"), "b1": ("sbuf", [128, 12], "int32"), "base": ("sbuf", [128, 12], "int32"),
    "m1": ("sbuf", [128, RO * NI], "bfloat16"), "m5": ("sbuf", [128, RO * NI], "bfloat16"),
    "dt": ("sbuf", [128, RO * 16], "int32"), "dl": ("sbuf", [128, RO * 16], "uint16"),
    "oys": ("sbuf", [128, NI], "float32"), "oyt": ("sbuf", [128, NI], "float32"),
}
for _n in ("off1", "off2", "off5", "zout", "zin", "zret", "zback"):
    SCRATCH[_n] = ("sbuf", [128, RO * NI], "uint16")
for _n in ("so", "si", "to", "ti"):
    SCRATCH[_n] = ("sbuf", [128, RO * NI], "float16")
for _i in range(NB + 1):
    SCRATCH["tb%d" % _i] = ("sbuf", [128, W + 8], "float32" if _i else "int32")
for _i in range(NG):
    SCRATCH["gb%d" % _i] = ("sbuf", [128, B * NI], "float16")
for _i in range(8):
    SCRATCH["ps%d" % _i] = ("psum", [128, 512], "float32")


def cost(o, m):
    k, n, q = o["k"], o["n"], o["q"]
    cy = 0.00083 * m["f"]
    if k == "gather":
        d = (0.05 if q == "V" else 0.065) + n * m["cg"] * cy
    elif k == "scatter":
        d = 0.05 + n * m["cs"] * cy
    elif k == "ew":
        d = (0.17 + 2 * n * cy) if q == "P" else 0.04 + max(64, n) * cy
    elif k == "mm":
        d = n * m["pe"] * 0.001 * m["f"]
    elif k == "send":
        hold = m["iss"] + m["first"] * o["first"]
        return hold, hold + m[o["via"]] + m["first"] * o["first2"]
    elif k == "dma":
        return 0.1, m["dma0"] + n / m["bw"] * 0.001
    return d, d + m["wake"]


def build(c):
    ops = []
    ON = c["ON"]

    def op(name, q, k, n, deps, **kw):
        o = dict(name=name, q=q, k=k, n=n, deps=list(deps), pre=None, i=len(ops), pos=-1.0)
        o.update(kw)
        ops.append(o)
        return o

    def ew(name, q, n, deps, **kw):
        return op(name, q, "ew", n, deps, **kw)

    def over(parts, a, b):
        return [o for x, y, o in parts if x < b and a < y]

    def place(t, st):
        return c["AT"].get(10 * t + st) or (c["ST"][st][0], c["ST"][st][1] + 10 * t, c["ST"][st][2])

    def chunks(t, st):
        return FORM[place(t, st)[0]]

    z2 = ew("zero_eye", "V", 128, [], do=("zero_eye",), pos=-9.0)
    eye = ew("eye", "P", 256, [z2], do=("eye",), pos=-9.0)
    io0 = ew("io0", "P", 12, [], do=("io0",), pos=-8.0)
    io1 = ew("io1", "P", 12, [], do=("io1",), pos=-8.0)
    z1 = ew("zero_dm", "V", 64, [], do=("zero_dm",), pos=-8.0)
    io2 = ew("io2", "P", 16, [], do=("io2",), pos=-10.0)
    ma = ew("ma", "V", 16, [io2], do=("ma",), pos=-9.0)
    mb = ew("mb", "V", 16, [ma], do=("mb",), pos=-9.0)
    dms = [ew("dm%d" % j, "APV"[j % 3], 64 if j % 3 == 2 else 128, [eye] if j % 3 == 1 else [eye, mb], do=("dm", j), pos=-4.0)
           for j in range(B)]
    dm = op("dm", "E", "mm", 0, dms + [z1], do=("none",))
    ba = ew("ba", "V", 12, [io0], do=("ba",))
    base = ew("base", "V", 24, [ba, io1], do=("base",))
    eye32 = ew("eye32", "P", 256, [eye], do=("eye32",))
    rot0 = ew("rot0", "P", 256, [eye], do=("rot0",))
    rot = ew("rot", "P", 16, [rot0], do=("rot",))
    one = ew("one", "V", 64, [], do=("one",))
    kc = []
    for rows, value in ((4, 2 * MID), (3, MID), (2, 0.25), (1, BIG)):
        kc = [ew("kc%d" % rows, "V", 64, kc, do=("kc", rows, value))]
    LD = [((x + H // 2) % H, (y + H // 2 - 1) % H + 1) for x, y in zip(c["LD"][:-1], c["LD"][1:])]
    lds, un, chain, done = [], [], [], 0
    for j, (x, y) in enumerate(LD):
        done += 512 * (y - x)
        lds.append(op("ld%d" % j, "S", "dma", done, [], do=("ld", x, y), sem="ld%d" % j))
        chain.append(lds[-1])
        if j == c["SA"]:
            done += 512 * NI
            lsa = op("ldsa", "S", "dma", done, [], do=("ldsa",), sem="ldsa")
            chain.append(lsa)
    lta = op("ldta", "S", "dma", done + 512 * NI, [], do=("ldta",), sem="ldta")
    for x, y in zip(chain, chain[1:] + [lta]):
        y["pre"] = x
    for j, (x, y) in enumerate(LD):
        un.append((x, y, ew("lo%d" % j, "V", y - x, [lds[j]], do=("lo", x, y), pos=-5.0)))
        if j in c["AH"]:
            h = ew("hj%d" % j, "A", y - x, [lds[j]], do=("hj", x, y), pos=-5.0)
            un.append((H + x, H + y, ew("hk%d" % j, "A", y - x, [h], do=("hk", x, y), pos=-6.0)))
        else:
            un.append((H + x, H + y, ew("hi%d" % j, "V", y - x, [lds[j]], do=("hi", x, y), pos=-5.0)))
    made = {0: [o for _, _, o in un]}
    cp1 = [(x, y, ew("cp1_%d" % x, ("PA" if j < 8 else "VA")[j % 2], y - x, [o], do=("cp", 1, 0, x, y),
                     pos=-0.4 + (x >= B * NI), row=j >= 8)) for j, (x, y, o) in enumerate(un)]
    t16 = ew("t16", "A", NI, [lta], do=("t16",), pos=-0.3, row=True)
    dl, sarr, tarr = {}, {}, {}

    def lookup(t, st, a, b, deps, win, opened=None):
        form, at, gap = place(t, st)
        pos = at + gap * FORM[form].index((a, b))
        mid = a + 2 * int(round(c["SH"][st] * (b - a) / 2))
        gs = [op("g%d%d_%d%s" % (t, st, x, q), q, "gather", B * (y - x), deps + made[t], stage=(t, st), cols=(x, y),
                 win=win, pos=pos, row=True, reads=t) for x, y, q in ((a, mid, "A"), (mid, b, "V"))]
        e = op("e%d%d_%d_%d" % (t, st, a, a), "E", "mm", B * max(64, b - a), gs + [dm] + ([opened] if opened else []),
               stage=(t, st), cols=(a, b), do=("ext", opened is None), pos=pos - 100)
        if opened is None:
            e["bank"] = e["rb"] = e["name"]
        else:
            e["same"], e["rb"] = opened, opened["rb"]
        return gs, e, e["rb"]

    def sends(kind, t, srcs, via):
        return [(a, b, op("send_%s%d_%d" % (kind, t, a), "P", "send", 0, [o], via=via,
                          first=int(kind == "s" and t == 1 and a == srcs[0][0]), first2=int(via == "rel" and t == 1 and a == srcs[0][0]),
                          pos="zsyt".index(kind) - 5.0, do=("send", kind, t, a, b), sem="%s%d_%d" % (kind, t, a))) for a, b, o in srcs]

    def remainder(nm, t, a, b, src, bank, buf, off):
        i1 = ew(nm + "a", ON["q" + buf[1]], b - a, [src], rb=bank, do=("conv", buf, t, a, b, -MID))
        return ew(nm + "b", "V", b - a, [i1], rb=bank, do=("rem", buf, off, t, a, b))

    def bring(v):
        x = v - 1
        if v == 1:
            cps, rest = over(cp1, 0, B * NI), over(cp1, B * NI, W)
        else:
            cps = []
            for j, y in enumerate(range(0, B * NI, PIECE)):
                kw = dict(do=("cp", v, x, y, y + PIECE), pos=10 * v - 15, reads=x)
                if v > 2 and j % 3 == 2:
                    cps.append(op("vc%d_%d" % (v, y), "S", "dma", 512 * PIECE, made[x][:1] + cps[-1:], sem="vc%d_%d" % (v, y), **kw))
                else:
                    cps.append(ew("vc%d_%d" % (v, y), "P", PIECE, made[x][:1], **kw))
            if v > NB:
                rest = []
                for o in cps:
                    o["deps"] += [u for u in ops if u.get("reads") == v - NB]
            else:
                src = over(cp1, B * NI, W) + made[max(1, v - 2)][:1]
                rest = [op("tl%d" % v, "S", "dma", 512 * (W - B * NI), src, do=("cp", v, 1, B * NI, W), sem="tl%d" % v)]
        cc = op("bcol%d" % x, ON["bcol"], "gather", NI, [dl[x]] + made[x][:1] + cps, do=("bcol", x), reads=x)
        made[v] = [op("scat%d" % x, "V", "scatter", NI, [cc], do=("scat", x), reads=x)] + rest

    for t in range(RO):
        if t:
            bring(t)
        wrap = ew("wrap%d" % t, "P", 1, made[t][:1] if t else over(un, 0, 1), do=("wrap", t), pos=1.0, reads=t)
        g1, c1u, c1h, c2, c3, c4, c5 = [], [], [], [], [], [], []
        for a, b in chunks(t, 1):
            nm = "%d_%d" % (t, a)
            if t == 0:
                i1 = ew("i1a" + nm, "V", 2 * (b - a), [lsa] + over(un, B * a, B * b), do=("sum0", a, b), pos=-5.5 + 100 * bool(g1))
                i2 = ew("i1b" + nm, "V", b - a, [i1], do=("and", a, b), pos=-5.6 + 100 * bool(g1))
                i3 = ew("i1c" + nm, "A", b - a, [i2], do=("tou", a, b), pos=-7.0)
            elif not g1:
                ms = op("mms" + nm, "E", "mm", 6 * NI, over(sarr[t], 0, NI) + made[t][:1] + [eye, eye32, one] + kc,
                        bank="mms" + nm, rb="mms" + nm, do=("mms", t, 0, NI), pos=-300.0, reads=t)
                i3 = remainder("i1" + nm, t, 0, NI, ms, ms["bank"], "m1", "off1")
            gs, e, bank = lookup(t, 1, a, b, [i3], ("off1", W))
            g1 += gs
            c1u.append((a, b, ew("c1u" + nm, ON["c1u"], b - a, [e], rb=bank, do=("conv", "off2", t, a, b, MID), pos=-2.0)))
            if t == 0:
                c1h.append((a, b, ew("c1h" + nm, ON["c1h"], b - a, [e], rb=bank, do=("conv", "so", t, a, b, 0.0), pos=-3.0)))
        if t == RO - 1:
            c1h = [(0, NI, ew("c1h%d" % t, "V", NI, over(c1u, 0, NI), do=("half", "oys", t, 0, NI, 0.0), pos=99.0))]
            op("stys", "S", "dma", 512 * NI, over(c1h, 0, NI), do=("st", "ys", 0, NI), sem="stys")
        else:
            if t:
                c1h = [(0, NI, ew("c1h%d" % t, "V", NI // 2, over(c1u, 0, NI), do=("half", "so", t, 0, NI, -MID), pos=-3.0))]
            sarr[t + 1] = sends("s", t + 1, c1h, "rel")
            dmm = op("dmm%d" % t, "E", "mm", B * 64, g1 + [dm], stage=(t, 1), bank="dmm%d" % t, rb="dmm%d" % t, do=("dmm",), pos=-200.0)
            d1 = ew("d1_%d" % t, ON["d1"], 12, [dmm], rb=dmm["bank"], do=("d1", t))
            d2 = ew("d2_%d" % t, "V", 12, [d1], do=("d2", t))
            dl[t] = ew("d3_%d" % t, "V", 24, [d2, base], do=("d3", t))
        for a, b in chunks(t, 2):
            gs, e, bank = lookup(t, 2, a, b, over(c1u, a, b), ("off2", W))
            c2.append((a, b, ew("c2%d_%d" % (t, a), ON["c2"], b - a, [e], rb=bank, do=("conv", "zout", t, a, b, MID))))
        za = sends("z", t, c2, "hop")
        for a, b in chunks(t, 3):
            gs, e, bank = lookup(t, 3, a, b, over(za, a, b), ("zin", W))
            c3.append((a, b, ew("c3%d_%d" % (t, a), ON["c3"], b - a, [e], rb=bank, do=("conv", "zret", t, a, b, MID + 1))))
        zb = sends("y", t, c3, "hop")
        for a, b in chunks(t, 4):
            nm = "%d_%d" % (t, a)
            src = over(tarr[t], a, b) if t else [t16]
            mk = op("mmk" + nm, "E", "mm", max(64, b - a), [one] + kc, bank="mmk" + nm, rb="mmk" + nm, do=("mmk", a, b), pos=-400.0)
            gs, e, bank = lookup(t, 4, a, b, over(zb, a, b) + [wrap], ("zback", W + 1), mk)
            mk["deps"] = gs[:1] + mk["deps"]
            mt = op("mmt" + nm, "E", "mm", max(64, b - a), src + [rot, e], same=e, rb=bank, do=("mmt", t, a, b), pos=-300.0)
            c4.append((a, b, remainder("i5" + nm, t, a, b, mt, bank, "m5", "off5")))
        for a, b in chunks(t, 5):
            nm = "%d_%d" % (t, a)
            gs, e, bank = lookup(t, 5, a, b, over(c4, a, b), ("off5", W))
            if t < RO - 1:
                c5.append((a, b, ew("c5" + nm, ON["c5"], b - a, [e], rb=bank, do=("conv", "to", t, a, b, 0.0))))
            else:
                x = ew("c5" + nm, ON["c5"], b - a, [e], rb=bank, do=("conv", "oyt", 0, a, b, MID))
                op("styt%d" % a, "S", "dma", 512 * (b - a), [x], do=("st", "yt", a, b), sem="styt%d" % a)
        if t < RO - 1:
            tarr[t + 1] = sends("t", t + 1, c5, "rel")
    for o in ops:
        nm = o["name"]
        key = None
        if nm[:3] in ("c1u", "c1h") or nm[:2] in ("c2", "c3", "c5"):
            x = 3 if nm[:2] == "c1" else 2
            t, key = int(nm[x]), nm[:x] + "ab"[nm[x + 2:] not in ("0", "")]
        elif nm[:2] in ("i1", "i5") and nm[2].isdigit():
            t, key = int(nm[2]), "qr"[nm[-1] == "b"] + nm[1] + "ab"[nm[4:-1] != "0"]
        elif nm[:2] in ("d1", "d2", "d3") or nm[:4] in ("bcol", "scat"):
            t, key = int(nm[-1]), nm[:2] if nm[0] == "d" else nm[:4]
        if key in c["PAT"] and 1 <= t + (key[1] == "5") <= 4:
            q, at = c["PAT"][key]
            o["q"], o["pos"], o["row"] = q, 10 * t + at + 0.0001 * o["i"] / len(ops), True
    for q in "AV":
        row = sorted((o for o in ops if o["q"] == q and o.get("row")), key=lambda o: o["pos"])
        for x, y in zip(row, row[1:]):
            y["pre"] = x
    return ops


def schedule(c):
    ops = build(c)
    users = [[] for _ in ops]
    use = {}
    for o in ops:
        o["t1"] = None
        for d in o["deps"]:
            users[d["i"]].append(o)
        for key in ("stage", "rb"):
            if key in o:
                use.setdefault(o[key], []).append(o)
    slot = {}
    own = {"stage": [[] for _ in range(NG)], "rb": [[] for _ in range(8)]}
    free = {q: 0.0 for q in "AVPES"}
    left = [len(o["deps"]) for o in ops]
    ready, done = [], []

    def arrive(o):
        o["r"] = max([(d["te"] if d is o.get("same") else d["t1"]) for d in o["deps"]] + [0.0])
        ready.append(o)

    def earliest(o):
        extra, take = [], None
        key = "rb" if "bank" in o else "stage" if o["k"] == "gather" and "stage" in o else None
        if key and o[key] not in slot:
            can = [(max([u["t1"] for u in us] + [0.0]), s) for s, us in enumerate(own[key]) if all(u["t1"] is not None for u in us)]
            if not can:
                return None
            take = (key, min(can)[1])
            extra = [u for u in own[key][take[1]] if u["k"] != "gather"]
        elif key:
            extra = slot[o[key]][1]
        elif "rb" in o and "same" not in o:
            extra = [u for u in use[o["rb"]] if u["t1"] is not None and u["q"] != o["q"]]
        return max([o["r"]] + [u["t1"] for u in extra]), extra, take

    for o in ops:
        if not o["deps"]:
            arrive(o)
    while ready:
        cand = []
        for o in ready:
            if o["pre"] is None or o["pre"]["t1"] is not None:
                e = earliest(o)
                if e is not None:
                    cand += [(max(e[0], free[q]), q, o, e) for q in o["q"]]
        t0, q = min((x[0], x[1]) for x in cand)
        look = c["lookp"] if q == "P" else 0.0
        s, q, o, e = min((x for x in cand if x[1] == q and x[0] <= t0 + c["wait"].get(x[2].get("do", "g")[0], look)),
                         key=lambda x: (x[2]["pos"], x[2]["i"]))
        o["q"], o["t0"] = q, s
        hold, fin = cost(o, c)
        o["te"], o["t1"] = s + hold, s + fin
        free[q] = o["te"]
        o["deps"] = o["deps"] + [u for u in e[1] if all(u is not d for d in o["deps"])]
        if e[2] is not None:
            key, x = e[2]
            own[key][x] = use[o[key]]
            slot[o[key]] = (x, e[1])
        ready.remove(o)
        done.append(o)
        for u in users[o["i"]]:
            left[u["i"]] -= 1
            if not left[u["i"]]:
                arrive(u)
    for o in done:
        if "stage" in o:
            o["g"] = slot[o["stage"]][0]
        if "rb" in o:
            o["ps"] = slot[o["rb"]][0]
    done.sort(key=lambda x: x["t0"])
    return done


PLAN = schedule(CFG)
SEMAPHORES = ["qA", "qV", "qP", "qE", "left"] + [o["sem"] for o in PLAN if "sem" in o]
LAND = {"z": ("zout", "zin"), "y": ("zret", "zback"), "s": ("so", "si"), "t": ("to", "ti")}


def relay_of(topo, T, src, dst, kind):
    if topo.may_write(src, dst):
        return None
    can = [x for x in topo.cores_of(src) if T.rank_of(x) is None and topo.die(x) == topo.die(src) and topo.may_write(x, dst)]
    return can[0] if kind == "s" else can[-1]


def engines_of(topo, o, src, dst, far):
    e = topo.engines(src, far if o["do"][1:3] == ("s", 1) else dst)
    return sum(1 << x for x in e), len(e)


def rank_program(g, core, T, topo):
    N = len(T.cores)
    S = T.sem
    rank = T.rank_of(core)
    if rank is None:
        for r in range(N):
            src, dst = T.cores[r], T.cores[(r + 1) % N]
            mine = [kind for kind in "st" if relay_of(topo, T, src, dst, kind) == core]
            if mine:
                mask, ne = topo.mask(core, dst), len(topo.engines(core, dst))
                rid, pid = topo.addr(dst, core)
                tot = 0
                for o in PLAN:
                    if o["k"] == "send" and o["do"][1] in mine:
                        _, kind, t, a, b = o["do"]
                        ap = T[LAND[kind][1]][:, t * NI + a:t * NI + b]
                        g.wait_ge(S[o["sem"]], engines_of(topo, o, src, core, T.cores[(r + DQ) % N])[1])
                        g.remote_dma(ap, ap, S[o["sem"]], S.left, pid, rid, mask)
                        tot += ne
                g.wait_ge(S.left, tot)
        return
    nxt, prv, par = T.cores[(rank + 1) % N], T.cores[(rank - 1) % N], T.cores[(rank + DQ) % N]
    to = {"z": par, "y": par}
    gain = {"z": len(topo.engines(par, core)), "y": len(topo.engines(par, core))}
    for kind in "st":
        rel, rin = relay_of(topo, T, core, nxt, kind), relay_of(topo, T, prv, core, kind)
        to[kind] = nxt if rel is None else rel
        gain[kind] = len(topo.engines(prv if rin is None else rin, core))
    Q = {"A": g.scalar, "V": g.vector, "P": g, "E": g.tensor, "S": g.sync}
    V, PE = g.vector, g.tensor

    def sl(name, t, a, b):
        t = t if T[name].shape[1] > NI else 0
        return T[name][:, t * NI + a:t * NI + b]

    def tb(v):
        return T["tb%d" % (v if v <= NB else v - NB)]

    def affine(q, out, in_, add):
        if q == "A":
            return g.scalar.activation(out, in_, AF.Identity, bias=float(add)) if add else g.scalar.activation(out, in_, AF.Copy)
        if q == "P":
            return g.affine_select(out, in_, [[0, int(out.shape[1])]], AL.is_ge, 0.0, 0, 0)
        if q == "S":
            return g.sync.dma_start(out, in_)
        return V.tensor_scalar(out, in_, float(add), None, AL.add) if add else V.tensor_copy(out, in_)

    def emit(o):
        q = o["q"]
        if o["k"] == "gather" and "stage" in o:
            t, (a, b), (off, w) = o["stage"][0], o["cols"], o["win"]
            return affine(q, T["gb%d" % o["g"]][:, B * a:B * b], tb(t)[:, 0:w].indirect(sl(off, t, a, b)), -MID)
        d = o["do"]
        k = d[0]
        ps = T["ps%d" % o["ps"]] if "ps" in o else None
        if k == "zero_dm":
            return V.memset(T.dm[:, 0:16], 0.0)
        if k == "zero_eye":
            return V.memset(T.eye2[:], 0.0)
        if k == "dm":
            out, col = T.dm[:, 16 + 128 * d[1]:144 + 128 * d[1]], T.mk[:, d[1]:d[1] + 1]
            if q == "A":
                return g.scalar.activation(out, T.eye2[:, 0:128], AF.Identity, scale=col)
            if q == "P":
                return g.affine_select(out, T.eye2[:, 0:128], [[0, 8], [1, B]], AL.is_equal, 0.0, -d[1], 0)
            return V.tensor_scalar(out, T.eye2[:, 0:128], col, None, AL.mult)
        if k == "io2":
            return g.iota(T.mi[:], [[-1, B]], B, 1)
        if k == "ma":
            return V.tensor_scalar(T.mi[:], T.mi[:], B - 1, None, AL.bitwise_and)
        if k == "mb":
            return V.tensor_scalar(T.mk[:], T.mi[:], 0.0, None, AL.is_equal)
        if k == "io0":
            return g.iota(T.b0[:], [[0, 12]], 0, B)
        if k == "io1":
            return g.iota(T.b1[:], [[B * B, 12]], 0, 0)
        if k == "ba":
            return V.tensor_scalar(T.b0[:], T.b0[:], B * B - 1, None, AL.bitwise_and)
        if k == "base":
            return V.tensor_tensor(T.base[:], T.b0[:], T.b1[:], AL.add)
        if k == "eye":
            return g.affine_select(T.eye2[:], T.eye2[:], [[0, 2], [-1, 128]], AL.not_equal, 1.0, 0, 1)
        if k == "eye32":
            return affine("P", T.eye32[:], T.eye2[:], 0)
        if k == "rot0":
            return g.affine_select(T.rot2[:], T.eye2[:], [[0, 2], [-1, 128]], AL.not_equal, 1.0, -1, 1)
        if k == "rot":
            return g.affine_select(T.rot2[:, 15:256:16], T.eye2[:, 15:256:16], [[0, 2], [-16, 8]], AL.not_equal, 1.0, 0, 1)
        if k == "ld":
            return g.sync.dma_start(T.pmb[:, d[1]:d[2]], T.pm[:, d[1]:d[2]])
        if k == "ldsa":
            return g.sync.dma_start(T.sab[:], T.sa[:])
        if k == "ldta":
            return g.sync.dma_start(T.tab[:], T.ta[:])
        if k == "st":
            return g.sync.dma_start(T[d[1]][:, d[2]:d[3]], T["o" + d[1]][:, d[2]:d[3]])
        if k == "lo":
            return V.tensor_scalar(T.tb0[:, d[1]:d[2]], T.pmb[:, d[1]:d[2]], W - 1, None, AL.bitwise_and)
        if k == "hi":
            return V.tensor_scalar(T.tb0[:, H + d[1]:H + d[2]], T.pmb[:, d[1]:d[2]], 12, None, AL.logical_shift_right)
        if k == "hj":
            return g.scalar.activation(T.tb0[:, H + d[1]:H + d[2]], T.pmb[:, d[1]:d[2]], AF.Identity,
                                       bias=2.0 ** -13 + 0.5 - MID, scale=1.0 / W)
        if k == "hk":
            return affine(q, T.tb0[:, H + d[1]:H + d[2]], T.tb0[:, H + d[1]:H + d[2]], MID - 1)
        if k == "cp":
            return affine(q, tb(d[1])[:, d[3]:d[4]], tb(d[2])[:, d[3]:d[4]], 0)
        if k == "one":
            return V.memset(T.one[0:4, :], 1.0)
        if k == "kc":
            return V.memset(T.kc[0:d[1], :], d[2])
        if k == "rem":
            _, name, off, t, a, b = d
            return V.tensor_tensor(sl(off, t, a, b), ps[:, 0:b - a], sl(name, t, a, b), AL.subtract)
        if k == "t16":
            return affine(q, sl("ti", 0, 0, NI), T.tab[:], -MID)
        if k == "wrap":
            return affine(q, tb(d[1])[:, W:W + 1], tb(d[1])[:, 0:1], 0)
        if k == "sum0":
            return V.tensor_tensor(T.m0[:, d[1]:d[2]], T.sab[:, d[1]:d[2]], T.tb0[:, B * d[1]:B * d[2]:B], AL.add)
        if k == "and":
            return V.tensor_scalar(T.m0[:, d[1]:d[2]], T.m0[:, d[1]:d[2]], W - 1, None, AL.bitwise_and)
        if k == "tou":
            return affine(q, T.off1[:, d[1]:d[2]], T.m0[:, d[1]:d[2]], 0)
        if k == "mms":
            _, t, a, b = d
            PE.matmul(ps[:, 0:b - a], T.eye2[:, 128 - B * GS:256 - B * GS], sl("si", t, a, b), True, False)
            PE.matmul(ps[:, 0:b - a], T.one[0:3, :], T.kc[0:3, 0:b - a], False, False)
            return PE.matmul(ps[:, 0:b - a], T.eye32[:, 0:128], tb(t)[:, B * a + t:B * b:B], False, True)
        if k == "mmk":
            return PE.matmul(ps[:, 0:d[2] - d[1]], T.one[0:4, :], T.kc[0:4, 0:d[2] - d[1]], True, False)
        if k == "mmt":
            _, t, a, b = d
            x = 128 - B * GS if t else 0
            return PE.matmul(ps[:, 0:b - a], T.rot2[:, x:x + 128], sl("ti", t, a, b), False, True)
        if k == "ext":
            a, b = o["cols"]
            for j in range(B):
                r = PE.matmul(ps[:, 0:b - a], T.dm[:, 16 + 128 * j:144 + 128 * j], T["gb%d" % o["g"]][:, B * a + j:B * b:B],
                              d[1] and j == 0, d[1] and j == B - 1)
            return r
        if k == "dmm":
            for j in range(B):
                r = PE.matmul(ps[:, 0:12], T.dm[:, 16 - j:144 - j], T["gb%d" % o["g"]][:, B * j:B * NI:B * B], j == 0, j == B - 1)
            return r
        if k == "conv":
            _, name, t, a, b, add = d
            return affine(q, sl(name, t, a, b), ps[:, 0:b - a], add)
        if k == "half":
            _, name, t, a, b, add = d
            return affine(q, sl(name, t, a, b), sl("off2", t, a, b), add)
        t = d[1]
        lst = T.dl[:, 16 * t:16 * t + 12]
        if k == "d1":
            return affine(q, T.dt[:, 16 * t:16 * t + 12], ps[:, 0:12], MID)
        if k == "d2":
            ap = T.dt[:, 16 * t:16 * t + 12]
            return V.tensor_scalar(ap, ap, B - 1, None, AL.bitwise_and)
        if k == "d3":
            return V.tensor_tensor(lst, T.dt[:, 16 * t:16 * t + 12], T.base[:], AL.add)
        if k == "bcol":
            return affine(q, tb(t + 1)[:, t:B * NI:B], tb(t)[:, 0:B * NI].indirect(lst), 0)
        if k == "scat":
            return V.tensor_copy(tb(t + 1)[:, 0:B * NI].indirect(lst), tb(t)[:, t:B * NI:B])
        raise ValueError(k)

    count = {q: 0 for q in "AVPE"}
    mark, clock = {}, {}
    known = {q: {} for q in Q}
    waited = set()
    sent = 0

    def wait(q, name, val, ck):
        if known[q].get(name, 0) < val:
            Q[q].wait_ge(S[name], val)
            waited.add((name, val))
            known[q][name] = val
            for n2, v2 in ck.items():
                if known[q].get(n2, 0) < v2:
                    known[q][n2] = v2

    for o in PLAN:
        q = o["q"]
        for d in sorted(o["deps"], key=lambda x: -x["t1"]):
            if d is not o.get("same") and mark[d["i"]]:
                wait(q, mark[d["i"]][0], mark[d["i"]][1], clock[d["i"]])
        if o.get("do") == ("none",):
            mark[o["i"]] = None
        elif o["k"] == "send":
            _, kind, t, a, b = o["do"]
            ts = t - 1 if o["via"] == "rel" else t
            rid, pid = topo.addr(to[kind], core)
            mask, ne = engines_of(topo, o, core, to[kind], par)
            g.remote_dma(sl(LAND[kind][1], t, a, b), sl(LAND[kind][0], ts, a, b), S[o["sem"]], S.left, pid, rid, mask)
            sent += ne
            mark[o["i"]], clock[o["i"]] = (o["sem"], gain[kind]), {}
        elif o["k"] == "dma":
            emit(o).then_inc(S[o["sem"]], 16)
            mark[o["i"]], clock[o["i"]] = (o["sem"], 16), dict(known[q])
        else:
            emit(o).then_inc(S["q" + q], 1)
            count[q] += 1
            mark[o["i"]], clock[o["i"]] = ("q" + q, count[q]), dict(known[q])
    g.wait_ge(S.left, sent)
    for q in "AVPE":
        g.wait_ge(S["q" + q], count[q])
    for o in PLAN:
        if "sem" in o and mark[o["i"]] not in waited:
            g.sync.wait_ge(S[o["sem"]], mark[o["i"]][1])
